import numpy as np
import ml_dtypes


def mxq(x, axis, fmt="e4m3"):
    dtype, down = {"e4m3": (ml_dtypes.float8_e4m3fn, 7), "e5m2": (ml_dtypes.float8_e5m2, 14)}[fmt]
    v = np.moveaxis(np.asarray(x, np.float32).astype(ml_dtypes.bfloat16).astype(np.float64), axis, -1)
    blocks = v.reshape(v.shape[:-1] + (-1, 32))
    amax = np.abs(blocks).max(-1, keepdims=True)
    byte = np.maximum(np.where(amax > 0, np.frexp(amax)[1] - 1 + 127, 0) - down, 1)
    scale = np.exp2(byte - 127.0)
    codes = (blocks / scale).astype(np.float32).astype(dtype).astype(np.float64)
    return np.moveaxis((codes * scale).reshape(v.shape), -1, axis)


WIDE = False


def mx_kscale(k):
    if not WIDE:
        return np.ones(k)
    levels = np.array([10, -10, 5, -5, 0])
    if k % 512:
        return np.exp2(np.random.permutation(np.resize(levels, k // 32))).repeat(32)
    a = np.empty((k // 512, 16))
    for p in range(k // 512):
        a[p, :8] = np.random.permutation(np.resize(levels, 8))
        for g in range(8):
            far = levels[np.abs(levels - a[p, g]) >= 10]
            a[p, g + 8] = far[np.random.randint(len(far))]
    return np.exp2(a.ravel()).repeat(32)


def f64(x):
    return np.asarray(x).astype(np.float64)


def striped(idx):
    return np.tile(idx.reshape(-1, 16).T, (8, 1)).astype(np.uint16)


def unstriped(offs):
    return offs[:16].T.reshape(-1).astype(np.int64)


def striped8(idx):
    return np.concatenate([x.reshape(-1, 16).T for x in idx]).astype(np.uint16)


def runs(offs, k):
    lists = np.stack([offs[16 * r : 16 * r + 16].T.reshape(-1) for r in range(8)]).astype(np.int64)
    return lists[np.arange(k) % 512 // 64]


def pack_weight(w):
    k, n = w.shape
    w = f64(np.asarray(w, np.float32).astype(ml_dtypes.bfloat16)).reshape(k // 32, 32, n)
    amax = np.abs(w).max(1)
    byte = np.clip(np.where(amax > 0, np.frexp(amax)[1] - 1 + 127 - 7, 1), 1, 254)
    scaled = (w * np.exp2(127.0 - byte)[:, None, :]).reshape(k, n).astype(np.float32)
    words = np.ascontiguousarray(scaled.reshape(k // 512, 128, 4, n).transpose(0, 1, 3, 2)).astype(ml_dtypes.float8_e4m3fn).view(np.uint8)
    return words, np.ascontiguousarray(byte.astype(np.uint8).reshape(k // 512, 16, n))


def unpack_weight(words, scales):
    g, p, n, _ = words.shape
    vals = np.ascontiguousarray(words).view(ml_dtypes.float8_e4m3fn).astype(np.float64) * np.repeat(np.exp2(scales.astype(np.float64) - 127.0), 8, axis=1)[..., None]
    return vals.transpose(0, 1, 3, 2).reshape(g * 512, n)


E2M1 = np.array([0.0, 0.5, 1.0, 1.5, 2.0, 3.0, 4.0, 6.0, -0.0, -0.5, -1.0, -1.5, -2.0, -3.0, -4.0, -6.0])


def pack_fp4(w):
    k, n = w.shape
    w = f64(np.asarray(w, np.float32).astype(ml_dtypes.bfloat16)).reshape(k // 32, 32, n)
    amax = np.abs(w).max(1)
    mant, ex = np.frexp(amax / 6.0)
    byte = np.clip(np.where(amax > 0, np.where(mant > 0.5, ex, ex - 1) + 127, 1), 1, 254)
    scaled = (w * np.exp2(127.0 - byte)[:, None, :]).reshape(k, n).astype(np.float32)
    c = np.ascontiguousarray(scaled.reshape(k // 512, 128, 4, n).transpose(0, 1, 3, 2)).astype(ml_dtypes.float4_e2m1fn).view(np.uint8) & 0xF
    words = (c[..., 0::2] | (c[..., 1::2] << 4)).reshape(k // 512, 128, 2 * n)
    return np.ascontiguousarray(words), np.ascontiguousarray(byte.astype(np.uint8).reshape(k // 512, 16, n))


def unpack_fp4(words, scales):
    g, _, n = scales.shape
    words = np.ascontiguousarray(words).reshape(g, 128, n, 2)
    nib = np.empty((g, 128, n, 4), np.uint8)
    nib[..., 0::2] = words & 0xF
    nib[..., 1::2] = words >> 4
    vals = E2M1[nib] * np.repeat(np.exp2(scales.astype(np.float64) - 127.0), 8, axis=1)[..., None]
    return vals.transpose(0, 1, 3, 2).reshape(g * 512, n)


def planes(y):
    n, m = y.shape
    v = y.astype(np.float32).astype(ml_dtypes.bfloat16).astype(np.float64).reshape(n // 32, 32, m)
    top = np.abs(v).max(1)
    byte = np.clip(np.where(top > 0, np.frexp(top)[1] - 1 + 127 - 7, 1), 1, 254)
    codes = (v * np.exp2(127.0 - byte)[:, None, :]).reshape(n, m).astype(np.float32).astype(ml_dtypes.float8_e4m3fn).view(np.uint8)
    words = codes.reshape(n // 512, 128, 4, m).transpose(0, 1, 3, 2)
    return np.ascontiguousarray(words), np.ascontiguousarray(byte.astype(np.uint8).reshape(n // 512, 16, m))


K, T, S, H, G = 512, 1024, 512, 512, 2048


def setup_inputs():
    n = np.random.standard_normal
    s = mx_kscale(K)[:, None]
    packed_xT = pack_weight(n((K, T)) * s)
    packed_w1 = pack_fp4(n((K, H)) / np.sqrt(K) / s)
    packed_w2 = pack_fp4(n((K, H)) / np.sqrt(K) / s)
    packed_dT = pack_weight(n((K, G)) / s)
    return {
        "x_words": packed_xT[0],
        "x_scales": packed_xT[1],
        "w1_words": packed_w1[0],
        "w1_scales": packed_w1[1],
        "w2_words": packed_w2[0],
        "w2_scales": packed_w2[1],
        "gs": (np.random.uniform(0.5, 1.5, (K, 1)) * s).astype(np.float32),
        "d_words": packed_dT[0],
        "d_scales": packed_dT[1],
        "offs": striped(np.random.permutation(T)[:S]),
        "two": striped(np.random.permutation(T)[:S]),
        "n1": striped8(np.stack([np.random.permutation(S) for _ in range(8)])),
        "n2": striped8(np.stack([np.random.permutation(S) for _ in range(8)])),
        "n3": striped8(np.stack([np.random.permutation(S) for _ in range(8)])),
        "k1": striped8(np.random.randint(0, G, (8, H))),
        "n4": striped8(np.stack([np.random.permutation(S) for _ in range(8)])),
        "n5": striped8(np.stack([np.random.permutation(S) for _ in range(8)])),
    }


def reference(x_words, x_scales, w1_words, w1_scales, w2_words, w2_scales, gs, d_words, d_scales, offs, two, n1, n2, n3, k1, n4, n5):
    d_k1 = unpack_weight(d_words, d_scales)[np.arange(K)[:, None], runs(k1, K)]
    x_two = unpack_weight(x_words, x_scales)[:, unstriped(two)]
    d = unpack_fp4(w2_words, w2_scales).T @ x_two
    xq = unpack_weight(x_words, x_scales)[:, unstriped(offs)]
    y = unpack_fp4(w1_words, w1_scales).T @ xq
    z = f64(gs) * (d * (y[np.arange(H)[:, None], runs(n1, H)] - y) + 0.5 * ((d[np.arange(H)[:, None], runs(n3, H)]) * (y[np.arange(H)[:, None], runs(n2, H)] - y)))
    h = 0.0625 * ((d_k1.T @ mxq(z, 0, "e4m3")))
    pa = h[np.arange(H)[:, None], runs(n4, H)]
    pb = h[np.arange(H)[:, None], runs(n5, H)]
    mu = 0.3125 * (h + pa + pb)
    out_0 = (h - mu) / (np.sqrt((pa - mu) ** 2 + (pb - mu) ** 2 + 0.25))
    return (out_0,) + planes(out_0)

@@ -1,0 +1,301 @@
+from contextlib import ExitStack
+
+import concourse.mybir as mybir
+from concourse.masks import make_identity
+
+K, T, S, H, G = 512, 1024, 512, 512, 2048
+FLOPS = 3 * 2 * K * H * S
+
+F32 = mybir.dt.float32
+BF16 = mybir.dt.bfloat16
+I32 = mybir.dt.int32
+U32 = mybir.dt.uint32
+U16 = mybir.dt.uint16
+U8 = mybir.dt.uint8
+FP8X4 = mybir.dt.float8_e4m3fn_x4
+FP4X4 = mybir.dt.float4_e2m1fn_x4
+ALU = mybir.AluOpType
+ACT = mybir.ActivationFunctionType
+
+P = 128
+PACK = 4
+BLOCKS = S // P
+PIECES = ((0, 256), (256, 128), (384, 128))
+Z_PIECES = ((0, 128), (128, 128), (256, 128), (384, 128))
+
+
+def tile_picked_twqflowbstd_none_po_kernel(
+    tc, x_words, x_scales, w1_words, w1_scales, w2_words, w2_scales, gs, d_words, d_scales,
+    offs, two, n1, n2, n3, k1, n4, n5, out_0, out_1, out_2,
+):
+    nc = tc.nc
+    with ExitStack() as ctx:
+        keep = ctx.enter_context(tc.tile_pool(name="keep", bufs=1))
+        ring = ctx.enter_context(tc.tile_pool(name="ring", bufs=3))
+        rows_psum = ctx.enter_context(tc.psum_pool(name="rows_psum", bufs=4))
+        left_psum = ctx.enter_context(tc.psum_pool(name="left_psum", bufs=1))
+        right_psum = ctx.enter_context(tc.psum_pool(name="right_psum", bufs=3))
+
+        def load_list(name, src):
+            tile = keep.tile([P, S // 16], U16, name=name)
+            nc.sync.dma_start(tile[:], src)
+            return tile
+
+        def entries(lst, start, n):
+            return lst[:, start // 16 : (start + n) // 16]
+
+        def zeroed_plane(name, width, engine):
+            tile = keep.tile([P, width], U8, name=name, align_bytes=64)
+            engine.memset(tile[:].bitcast(I32), 0)
+            return tile
+
+        def load_plane(tile, scales, places, engine):
+            rows = scales[0].bitcast(I32).rearrange("(q r) c -> r q c", r=4)
+            for r in range(4):
+                engine.dma_start(tile[places[r] : P : 32, :].bitcast(I32), rows[r])
+
+        def add_transposed(out, parts):
+            for i, part in enumerate(parts):
+                nc.tensor.matmul(out, part, ident[:], is_transpose=True, start=(i == 0), stop=(i == len(parts) - 1))
+
+        xs = zeroed_plane("xs", T, nc.gpsimd)
+        w1s = zeroed_plane("w1s", H, nc.vector)
+        ds = zeroed_plane("ds", G, nc.gpsimd)
+        w2s = zeroed_plane("w2s", H, nc.vector)
+        dk_scales = zeroed_plane("dk_scales", H, nc.vector)
+
+        offs_l = load_list("offs_l", offs)
+        xw = keep.tile([P, T], I32, name="xw")
+        nc.sync.dma_start(xw[:], x_words[0].rearrange("p c r -> p (c r)").bitcast(I32))
+        load_plane(xs, x_scales, (0, 1, 2, 3), nc.sync)
+        w1w = keep.tile([P, 2 * H], U8, name="w1w", align_bytes=64)
+        nc.sync.dma_start(w1w[:].bitcast(I32), w1_words[0].bitcast(I32))
+        two_l = load_list("two_l", two)
+        load_plane(w1s, w1_scales, (0, 1, 2, 3), nc.sync)
+        k1_l = load_list("k1_l", k1)
+        dw = keep.tile([P, G], I32, name="dw")
+        nc.sync.dma_start(dw[:], d_words[0].rearrange("p c r -> p (c r)").bitcast(I32))
+        load_plane(ds, d_scales, (0, 1, 16, 17), nc.gpsimd)
+        w2w = keep.tile([P, 2 * H], U8, name="w2w", align_bytes=64)
+        nc.sync.dma_start(w2w[:].bitcast(I32), w2_words[0].bitcast(I32))
+        load_plane(w2s, w2_scales, (0, 1, 2, 3), nc.sync)
+        n2_l = load_list("n2_l", n2)
+        n1_l = load_list("n1_l", n1)
+        gs_t = keep.tile([P, PACK], F32, name="gs_t")
+        nc.sync.dma_start(gs_t[:], gs.rearrange("(p t) o -> p (t o)", t=PACK))
+        n3_l = load_list("n3_l", n3)
+        n4_l = load_list("n4_l", n4)
+        n5_l = load_list("n5_l", n5)
+
+        sixteen = keep.tile([P, 1], F32, name="sixteen")
+        nc.gpsimd.memset(sixteen[:], 16.0)
+        quarter = keep.tile([P, 1], F32, name="quarter")
+        nc.scalar.activation(quarter[:], sixteen[:], ACT.Abs_reciprocal_sqrt)
+        ident = keep.tile([P, P], F32, name="ident")
+        make_identity(nc, ident[:])
+        y_win = [keep.tile([P, S], F32, name="y_win%d" % t) for t in range(PACK)]
+        half_gs = keep.tile([P, PACK], F32, name="half_gs")
+        nc.gpsimd.tensor_scalar(half_gs[:], gs_t[:], 0.5, 0.0, ALU.mult, ALU.add)
+
+        def pick(name, words, plane, lst, cuts):
+            pw = keep.tile([P, S], I32, name=name + "_w", align_bytes=64)
+            ps = keep.tile([P, S], U8, name=name + "_s", align_bytes=64)
+            for start, n in cuts:
+                nc.vector.tensor_copy(pw[:, start : start + n].bitcast(U32), words[:].bitcast(U32).indirect(entries(lst, start, n)))
+                nc.vector.tensor_copy(ps[:, start : start + n], plane[:].indirect(entries(lst, start, n)))
+            return pw, ps
+
+        xq_w, xq_s = pick("xq", xw, xs, offs_l, ((0, 256), (256, 256)))
+        xt_w, xt_s = pick("xt", xw, xs, two_l, ((0, 512),))
+        dg_w, dg_s = pick("dg", dw, ds, k1_l, ((0, 512),))
+        dealt_s = keep.tile([P, H], U8, name="dealt_s")
+        nc.vector.tensor_copy(dealt_s[:].rearrange("p (t m) -> p t m", t=PACK), dg_s[:].rearrange("p (m t) -> p t m", t=PACK))
+        dk_words = keep.tile([P, H], I32, name="dk_words", align_bytes=64)
+        nc.vector.tensor_copy(dk_words[:].rearrange("p (t m) -> p t m", t=PACK), dg_w[:].rearrange("p (m t) -> p t m", t=PACK))
+        for r, place in enumerate((0, 1, 16, 17)):
+            nc.sync.dma_start(dk_scales[r:P:32, :].bitcast(I32), dealt_s[place:P:32, :].bitcast(I32))
+
+        def project(name, pw, ps, ww, ws):
+            banks = [rows_psum.tile([P, S], F32, name="rows") for t in range(PACK)]
+            for j in range(BLOCKS):
+                cols = slice(j * P, (j + 1) * P)
+                acc = right_psum.tile([P, H], F32, name="work")
+                nc.tensor.matmul_mx(acc[:], pw[:, cols].bitcast(FP8X4), ps[:, cols], ww[:].bitcast(FP4X4), ws[:], start=True, stop=True)
+                turned = ring.tile([P, PACK, P], F32, name="turned")
+                nc.scalar.copy(turned[:], acc[:].rearrange("p (m t) -> p t m", t=PACK))
+                for t in range(PACK):
+                    nc.tensor.transpose(banks[t][:, cols], turned[:, t, :], ident[:])
+            return banks
+
+        y_banks = project("y", xq_w, xq_s, w1w, w1s)
+        y_plain = [keep.tile([P, S], F32, name="y_plain%d" % t) for t in range(PACK)]
+        for t in range(PACK):
+            nc.scalar.copy(y_win[t][:], y_banks[t][:])
+            if t < 2:
+                nc.scalar.copy(y_plain[t][:], y_banks[t][:])
+            else:
+                nc.sync.dma_start(y_plain[t][:], y_win[t][:])
+        d_banks = project("d", xt_w, xt_s, w2w, w2s)
+        d_win = [keep.tile([P, S], F32, name="d_win%d" % t) for t in range(PACK)]
+        for t in range(PACK):
+            nc.scalar.activation(d_win[t][:], d_banks[t][:], ACT.Copy, scale=half_gs[:, t : t + 1])
+
+        diff2 = keep.tile([P, PACK, S], F32, name="diff2")
+        for t in range(PACK):
+            for start in (0, S // 2):
+                cols = slice(start, start + S // 2)
+                nc.vector.tensor_tensor(diff2[:, t, cols], y_win[t][:].indirect(entries(n2_l, start, S // 2)), y_plain[t][:, cols], ALU.subtract)
+
+        z_codes = keep.tile([P, S], U32, name="z_codes", align_bytes=64)
+        z_scales = keep.tile([P, S], U8, name="z_scales", align_bytes=64)
+        h_banks = [rows_psum.tile([P, S], F32, name="rows") for t in range(PACK)]
+        h_win = [keep.tile([P, S], F32, name="h_win%d" % t) for t in range(PACK)]
+        h_x = [keep.tile([P, S], F32, name="h_x%d" % t) for t in range(PACK)]
+        h_k = [keep.tile([P, S], F32, name="h_k%d" % t) for t in range(PACK)]
+
+        def product(cols, t):
+            m = slice(t * P, (t + 1) * P)
+            nc.tensor.matmul_mx(h_banks[t][:, cols], dk_words[:, m].bitcast(FP8X4), dk_scales[:, m], z_codes[:, cols].bitcast(FP8X4), z_scales[:, cols], start=True, stop=True)
+
+        def scaled(dst, cols, t, factor):
+            nc.scalar.activation(dst[t][:, cols], h_banks[t][:, cols], ACT.Copy, scale=factor * 0.0625)
+
+        def quantise(j, z_in):
+            cols = slice(j * P, (j + 1) * P)
+            nc.vector.quantize_mx(z_codes[:, cols].bitcast(FP8X4), z_scales[:, cols], z_in[:].rearrange("p c t -> p (c t)"))
+
+        def multiply(j):
+            cols = slice(j * P, (j + 1) * P)
+            for t in range(PACK):
+                product(cols, t)
+            for t in range(PACK):
+                scaled(h_win, cols, t, 1.0)
+                scaled(h_x, cols, t, -2.2)
+                scaled(h_k, cols, t, 8.0 / 15.0)
+
+        def staged(shape, dtype):
+            return keep.tile(shape, dtype, name="stage", bufs=3, align_bytes=64)
+
+        for j in range(BLOCKS):
+            cols = slice(j * P, (j + 1) * P)
+            last = j == BLOCKS - 1
+            diff1 = [keep.tile([P, P], F32, name="diff1_%d" % t) for t in range(PACK)]
+            if last:
+                far = staged([P, PACK, P], F32)
+                z_in = staged([P, P, PACK], BF16)
+                own = staged([P, PACK, P], F32)
+            else:
+                own = staged([P, PACK, P], F32)
+                z_in = staged([P, P, PACK], BF16)
+                far = keep.tile([P, PACK, P], F32, name="far", bufs=2)
+            for t in range(PACK):
+                nc.vector.tensor_tensor(diff1[t][:], y_win[t][:].indirect(entries(n1_l, j * P, P)), y_plain[t][:, cols], ALU.subtract)
+            for step in ((1, 0) if last else (0, 1)):
+                for t in range(PACK):
+                    if step == 0:
+                        nc.vector.scalar_tensor_tensor(own[:, t, :], diff1[t][:], 2.0, d_win[t][:, cols], ALU.mult, ALU.mult)
+                    else:
+                        nc.vector.tensor_tensor(far[:, t, :], d_win[t][:].indirect(entries(n3_l, j * P, P)), diff2[:, t, cols], ALU.mult)
+            if not last:
+                zt = left_psum.tile([P, PACK, P], F32, name="zt", bufs=1)
+                for t in range(PACK):
+                    add_transposed(zt[:, t, :], [own[:, t, :], far[:, t, :]])
+                zb = ring.tile([P, 2, P, 2], BF16, name="zb")
+                nc.scalar.copy(zb[:], zt[:].rearrange("c (u e) m -> c u m e", e=2))
+                zw = right_psum.tile([P, 2, P], F32, name="work")
+                words = zb[:].rearrange("c u m e -> c (u m e)").bitcast(F32)
+                for u in range(2):
+                    nc.tensor.transpose(zw[:, u, :], words[:, u * P : (u + 1) * P], ident[:])
+                nc.scalar.copy(
+                    z_in[:].rearrange("p c t -> p (c t)").bitcast(F32).rearrange("p (c u) -> p c u", u=2),
+                    zw[:].rearrange("p u c -> p c u"),
+                )
+            else:
+                nc.vector.tensor_tensor(
+                    z_in[:].rearrange("p (c i) t -> p c t i", i=4),
+                    own[:].rearrange("p t (c i) -> p c t i", i=4),
+                    far[:].rearrange("p t (c i) -> p c t i", i=4),
+                    ALU.add,
+                )
+            quantise(j, z_in)
+            if 1 <= j < BLOCKS - 1:
+                multiply(j - 1)
+        before = slice(S - 2 * P, S - P)
+        final = slice(S - P, S)
+        both = slice(S - 2 * P, S)
+        for cols in (before, final):
+            for t in range(PACK):
+                product(cols, t)
+            for t in range(PACK):
+                scaled(h_win, cols, t, 1.0)
+                scaled(h_x, cols, t, -2.2)
+        for t in range(PACK):
+            scaled(h_k, both, t, 8.0 / 15.0)
+
+        out_rows = out_0.rearrange("(p t) c -> p t c", t=PACK)
+        out_words = out_1[0].rearrange("p c r -> p (c r)").bitcast(I32)
+        o_codes = keep.tile([P, S], I32, name="o_codes", align_bytes=64)
+        o_scales = keep.tile([P, S], U8, name="o_scales", align_bytes=64)
+        for start, n in PIECES:
+            cols = slice(start, start + n)
+            res = keep.tile([P, PACK, n], F32, name="res%d" % start)
+            for t0 in range(0, PACK, 2):
+                pair = (t0, t0 + 1)
+                q = dict((t, ring.tile([P, n], F32, name="q", bufs=4)) for t in pair)
+                r = dict((t, ring.tile([P, n], F32, name="r", bufs=4)) for t in pair)
+                num = dict((t, ring.tile([P, n], F32, name="num", bufs=4)) for t in pair)
+                for t in pair:
+                    nc.vector.tensor_tensor(q[t][:], h_win[t][:].indirect(entries(n4_l, start, n)), h_x[t][:, cols], ALU.add)
+                for t in pair:
+                    nc.vector.tensor_tensor(r[t][:], h_win[t][:].indirect(entries(n5_l, start, n)), q[t][:], ALU.subtract)
+                for t in pair:
+                    nc.vector.scalar_tensor_tensor(num[t][:], q[t][:], 2.0, r[t][:], ALU.mult, ALU.add)
+                if start + n < S:
+                    for t in pair:
+                        lin = rows_psum.tile([P, 2, n], F32, name="rows")
+                        for j in range(n // P):
+                            blk = slice(j * P, (j + 1) * P)
+                            src = slice(start + j * P, start + (j + 1) * P)
+                            add_transposed(lin[:, 0, blk], [h_x[t][:, src], r[t][:, blk]])
+                        for j in range(n // P):
+                            blk = slice(j * P, (j + 1) * P)
+                            src = slice(start + j * P, start + (j + 1) * P)
+                            add_transposed(lin[:, 1, blk], [h_k[t][:, src], num[t][:, blk]])
+                        sq = ring.tile([P, 2, n], F32, name="sq")
+                        nc.scalar.activation(sq[:, 0, :], lin[:, 0, :], ACT.Square, scale=0.5**0.5)
+                        nc.scalar.activation(sq[:, 1, :], lin[:, 1, :], ACT.Square, scale=0.375 * 0.5**0.5)
+                        tot = right_psum.tile([P, n], F32, name="work")
+                        for j in range(n // P):
+                            blk = slice(j * P, (j + 1) * P)
+                            add_transposed(tot[:, blk], [sq[:, 0, blk], sq[:, 1, blk]])
+                        inv = ring.tile([P, n], F32, name="inv")
+                        nc.scalar.activation(inv[:], tot[:], ACT.Abs_reciprocal_sqrt, bias=quarter[:])
+                        nc.vector.scalar_tensor_tensor(res[:, t, :], num[t][:], -0.3125, inv[:], ALU.mult, ALU.mult)
+                else:
+                    lin = dict((t, ring.tile([P, 2, n], F32, name="lin", bufs=4)) for t in pair)
+                    sq = dict((t, ring.tile([P, 2, n], F32, name="sq2", bufs=4)) for t in pair)
+                    tot = dict((t, ring.tile([P, n], F32, name="tot", bufs=4)) for t in pair)
+                    inv = dict((t, ring.tile([P, n], F32, name="inv2", bufs=4)) for t in pair)
+                    for t in pair:
+                        nc.vector.tensor_tensor(lin[t][:, 0, :], r[t][:], h_x[t][:, cols], ALU.add)
+                        nc.scalar.activation(sq[t][:, 0, :], lin[t][:, 0, :], ACT.Square, scale=0.5**0.5)
+                    for t in pair:
+                        nc.vector.tensor_tensor(lin[t][:, 1, :], num[t][:], h_k[t][:, cols], ALU.add)
+                        nc.scalar.activation(sq[t][:, 1, :], lin[t][:, 1, :], ACT.Square, scale=0.375 * 0.5**0.5)
+                    for t in pair:
+                        nc.vector.tensor_tensor(tot[t][:], sq[t][:, 0, :], sq[t][:, 1, :], ALU.add)
+                        nc.scalar.activation(inv[t][:], tot[t][:], ACT.Abs_reciprocal_sqrt, bias=quarter[:])
+                    for t in pair:
+                        nc.vector.scalar_tensor_tensor(res[:, t, :], num[t][:], -0.3125, inv[t][:], ALU.mult, ALU.mult)
+            nc.sync.dma_start(out_rows[:, :, cols], res[:])
+            o_in = keep.tile([P, n, PACK], BF16, name="o_in%d" % start, align_bytes=64)
+            dst = o_in[:].rearrange("p (c i) t -> p c t i", i=4)
+            src = res[:].rearrange("p t (c i) -> p c t i", i=4)
+            if start + n < S:
+                nc.scalar.copy(dst, src)
+            else:
+                nc.vector.tensor_copy(dst, src)
+            nc.vector.quantize_mx(o_codes[:, cols].bitcast(FP8X4), o_scales[:, cols], o_in[:].rearrange("p c t -> p (c t)"))
+            nc.sync.dma_start(out_words[:, cols], o_codes[:, cols])
+        for quad in range(4):
+            nc.sync.dma_start(out_2[0].bitcast(I32)[4 * quad : 4 * quad + 4, :], o_scales[32 * quad : 32 * quad + 4, :].bitcast(I32))

@@ -21,7 +21,9 @@ P = 128
 PACK = 4
 BLOCKS = S // P
 PIECES = ((0, 256), (256, 128), (384, 128))
-Z_PIECES = ((0, 128), (128, 128), (256, 128), (384, 128))
+Z_PIECES = ((0, 256), (256, 128), (384, 128))
+UNITS = ((0, 256, 0, 2, True, False), (0, 256, 2, 2, True, False), (256, 128, 0, 4, True, False), (384, 128, 0, 3, True, False), (384, 128, 3, 1, True, False))
+QB, NB, YS, ILV, LIN = 2, 3, 4, 0, 4
 
 
 def tile_picked_twqflowbstd_none_po_kernel(
@@ -49,10 +51,10 @@ def tile_picked_twqflowbstd_none_po_kernel(
             engine.memset(tile[:].bitcast(I32), 0)
             return tile
 
-        def load_plane(tile, scales, places, engine):
+        def load_plane(tile, scales, places, engines):
             rows = scales[0].bitcast(I32).rearrange("(q r) c -> r q c", r=4)
             for r in range(4):
-                engine.dma_start(tile[places[r] : P : 32, :].bitcast(I32), rows[r])
+                engines[r].dma_start(tile[places[r] : P : 32, :].bitcast(I32), rows[r])
 
         def add_transposed(out, parts):
             for i, part in enumerate(parts):
@@ -60,25 +62,26 @@ def tile_picked_twqflowbstd_none_po_kernel(
 
         xs = zeroed_plane("xs", T, nc.gpsimd)
         w1s = zeroed_plane("w1s", H, nc.vector)
-        ds = zeroed_plane("ds", G, nc.gpsimd)
+        ds = zeroed_plane("ds", G, nc.vector)
         w2s = zeroed_plane("w2s", H, nc.vector)
         dk_scales = zeroed_plane("dk_scales", H, nc.vector)
+        on_sync = (nc.sync,) * 4
 
         offs_l = load_list("offs_l", offs)
         xw = keep.tile([P, T], I32, name="xw")
         nc.sync.dma_start(xw[:], x_words[0].rearrange("p c r -> p (c r)").bitcast(I32))
-        load_plane(xs, x_scales, (0, 1, 2, 3), nc.sync)
+        load_plane(xs, x_scales, (0, 1, 2, 3), on_sync)
         w1w = keep.tile([P, 2 * H], U8, name="w1w", align_bytes=64)
         nc.sync.dma_start(w1w[:].bitcast(I32), w1_words[0].bitcast(I32))
         two_l = load_list("two_l", two)
-        load_plane(w1s, w1_scales, (0, 1, 2, 3), nc.sync)
+        load_plane(w1s, w1_scales, (0, 1, 2, 3), on_sync)
         k1_l = load_list("k1_l", k1)
         dw = keep.tile([P, G], I32, name="dw")
         nc.sync.dma_start(dw[:], d_words[0].rearrange("p c r -> p (c r)").bitcast(I32))
-        load_plane(ds, d_scales, (0, 1, 16, 17), nc.gpsimd)
+        load_plane(ds, d_scales, (0, 1, 16, 17), on_sync)
         w2w = keep.tile([P, 2 * H], U8, name="w2w", align_bytes=64)
         nc.sync.dma_start(w2w[:].bitcast(I32), w2_words[0].bitcast(I32))
-        load_plane(w2s, w2_scales, (0, 1, 2, 3), nc.sync)
+        load_plane(w2s, w2_scales, (0, 1, 2, 3), on_sync)
         n2_l = load_list("n2_l", n2)
         n1_l = load_list("n1_l", n1)
         gs_t = keep.tile([P, PACK], F32, name="gs_t")
@@ -108,10 +111,10 @@ def tile_picked_twqflowbstd_none_po_kernel(
         xq_w, xq_s = pick("xq", xw, xs, offs_l, ((0, 256), (256, 256)))
         xt_w, xt_s = pick("xt", xw, xs, two_l, ((0, 512),))
         dg_w, dg_s = pick("dg", dw, ds, k1_l, ((0, 512),))
-        dealt_s = keep.tile([P, H], U8, name="dealt_s")
-        nc.vector.tensor_copy(dealt_s[:].rearrange("p (t m) -> p t m", t=PACK), dg_s[:].rearrange("p (m t) -> p t m", t=PACK))
         dk_words = keep.tile([P, H], I32, name="dk_words", align_bytes=64)
         nc.vector.tensor_copy(dk_words[:].rearrange("p (t m) -> p t m", t=PACK), dg_w[:].rearrange("p (m t) -> p t m", t=PACK))
+        dealt_s = keep.tile([P, H], U8, name="dealt_s")
+        nc.vector.tensor_copy(dealt_s[:].rearrange("p (t m) -> p t m", t=PACK), dg_s[:].rearrange("p (m t) -> p t m", t=PACK))
         for r, place in enumerate((0, 1, 16, 17)):
             nc.sync.dma_start(dk_scales[r:P:32, :].bitcast(I32), dealt_s[place:P:32, :].bitcast(I32))
 
@@ -130,42 +133,32 @@ def tile_picked_twqflowbstd_none_po_kernel(
         y_banks = project("y", xq_w, xq_s, w1w, w1s)
         y_plain = [keep.tile([P, S], F32, name="y_plain%d" % t) for t in range(PACK)]
         for t in range(PACK):
-            nc.scalar.copy(y_win[t][:], y_banks[t][:])
-            if t < 2:
+            nc.scalar.copy(y_win[t][:, :S], y_banks[t][:])
+            if t < YS:
                 nc.scalar.copy(y_plain[t][:], y_banks[t][:])
             else:
-                nc.sync.dma_start(y_plain[t][:], y_win[t][:])
+                nc.sync.dma_start(y_plain[t][:], y_win[t][:, :S])
         d_banks = project("d", xt_w, xt_s, w2w, w2s)
         d_win = [keep.tile([P, S], F32, name="d_win%d" % t) for t in range(PACK)]
         for t in range(PACK):
             nc.scalar.activation(d_win[t][:], d_banks[t][:], ACT.Copy, scale=half_gs[:, t : t + 1])
 
-        diff2 = keep.tile([P, PACK, S], F32, name="diff2")
-        for t in range(PACK):
-            for start in (0, S // 2):
-                cols = slice(start, start + S // 2)
-                nc.vector.tensor_tensor(diff2[:, t, cols], y_win[t][:].indirect(entries(n2_l, start, S // 2)), y_plain[t][:, cols], ALU.subtract)
 
         z_codes = keep.tile([P, S], U32, name="z_codes", align_bytes=64)
         z_scales = keep.tile([P, S], U8, name="z_scales", align_bytes=64)
         h_banks = [rows_psum.tile([P, S], F32, name="rows") for t in range(PACK)]
         h_win = [keep.tile([P, S], F32, name="h_win%d" % t) for t in range(PACK)]
-        h_x = [keep.tile([P, S], F32, name="h_x%d" % t) for t in range(PACK)]
-        h_k = [keep.tile([P, S], F32, name="h_k%d" % t) for t in range(PACK)]
+        h_x = keep.tile([P, PACK, S], F32, name="h_x")
+        h_k = keep.tile([P, PACK, S], F32, name="h_k")
 
         def product(cols, t):
             m = slice(t * P, (t + 1) * P)
             nc.tensor.matmul_mx(h_banks[t][:, cols], dk_words[:, m].bitcast(FP8X4), dk_scales[:, m], z_codes[:, cols].bitcast(FP8X4), z_scales[:, cols], start=True, stop=True)
 
         def scaled(dst, cols, t, factor):
-            nc.scalar.activation(dst[t][:, cols], h_banks[t][:, cols], ACT.Copy, scale=factor * 0.0625)
+            nc.scalar.activation(dst[t][:, cols] if isinstance(dst, list) else dst[:, t, cols], h_banks[t][:, cols], ACT.Copy, scale=factor * 0.0625)
 
-        def quantise(j, z_in):
-            cols = slice(j * P, (j + 1) * P)
-            nc.vector.quantize_mx(z_codes[:, cols].bitcast(FP8X4), z_scales[:, cols], z_in[:].rearrange("p c t -> p (c t)"))
-
-        def multiply(j):
-            cols = slice(j * P, (j + 1) * P)
+        def multiply(cols):
             for t in range(PACK):
                 product(cols, t)
             for t in range(PACK):
@@ -173,53 +166,47 @@ def tile_picked_twqflowbstd_none_po_kernel(
                 scaled(h_x, cols, t, -2.2)
                 scaled(h_k, cols, t, 8.0 / 15.0)
 
-        def staged(shape, dtype):
-            return keep.tile(shape, dtype, name="stage", bufs=3, align_bytes=64)
-
-        for j in range(BLOCKS):
-            cols = slice(j * P, (j + 1) * P)
-            last = j == BLOCKS - 1
-            diff1 = [keep.tile([P, P], F32, name="diff1_%d" % t) for t in range(PACK)]
-            if last:
-                far = staged([P, PACK, P], F32)
-                z_in = staged([P, P, PACK], BF16)
-                own = staged([P, PACK, P], F32)
-            else:
-                own = staged([P, PACK, P], F32)
-                z_in = staged([P, P, PACK], BF16)
-                far = keep.tile([P, PACK, P], F32, name="far", bufs=2)
+        for i, (start, n) in enumerate(Z_PIECES):
+            cols = slice(start, start + n)
+            last = start + n == S
+            diffs = keep.tile([P, 2, PACK, n], F32, name="z_in0" if last else "diffs", align_bytes=64)
+            diff1 = [diffs[:, 0, t, :] for t in range(PACK)]
+            own = keep.tile([P, PACK, n], F32, name="own%d" % i)
+            z_in = keep.tile([P, n, PACK], BF16, name="z_in%d" % i, align_bytes=64)
+            far = keep.tile([P, PACK, n], F32, name="z_in1" if last else "far%d" % i, align_bytes=64)
+            diff2 = [diffs[:, 1, t, :] for t in range(PACK)]
             for t in range(PACK):
-                nc.vector.tensor_tensor(diff1[t][:], y_win[t][:].indirect(entries(n1_l, j * P, P)), y_plain[t][:, cols], ALU.subtract)
-            for step in ((1, 0) if last else (0, 1)):
+                nc.vector.tensor_tensor(diff2[t][:], y_win[t][:].indirect(entries(n2_l, start, n)), y_plain[t][:, cols], ALU.subtract)
+                nc.vector.tensor_tensor(diff1[t][:], y_win[t][:].indirect(entries(n1_l, start, n)), y_plain[t][:, cols], ALU.subtract)
+            for step in (0, 1):
                 for t in range(PACK):
                     if step == 0:
                         nc.vector.scalar_tensor_tensor(own[:, t, :], diff1[t][:], 2.0, d_win[t][:, cols], ALU.mult, ALU.mult)
                     else:
-                        nc.vector.tensor_tensor(far[:, t, :], d_win[t][:].indirect(entries(n3_l, j * P, P)), diff2[:, t, cols], ALU.mult)
+                        nc.vector.tensor_tensor(far[:, t, :], d_win[t][:].indirect(entries(n3_l, start, n)), diff2[t][:], ALU.mult)
             if not last:
-                zt = left_psum.tile([P, PACK, P], F32, name="zt", bufs=1)
-                for t in range(PACK):
-                    add_transposed(zt[:, t, :], [own[:, t, :], far[:, t, :]])
-                zb = ring.tile([P, 2, P, 2], BF16, name="zb")
-                nc.scalar.copy(zb[:], zt[:].rearrange("c (u e) m -> c u m e", e=2))
-                zw = right_psum.tile([P, 2, P], F32, name="work")
-                words = zb[:].rearrange("c u m e -> c (u m e)").bitcast(F32)
-                for u in range(2):
-                    nc.tensor.transpose(zw[:, u, :], words[:, u * P : (u + 1) * P], ident[:])
-                nc.scalar.copy(
-                    z_in[:].rearrange("p c t -> p (c t)").bitcast(F32).rearrange("p (c u) -> p c u", u=2),
-                    zw[:].rearrange("p u c -> p c u"),
-                )
+                for j in range(n // P):
+                    blk = slice(j * P, (j + 1) * P)
+                    zt = left_psum.tile([P, PACK, P], F32, name="zt", bufs=1)
+                    for t in range(PACK):
+                        add_transposed(zt[:, t, :], [own[:, t, blk], far[:, t, blk]])
+                    zb = ring.tile([P, 2, P, 2], BF16, name="zb")
+                    nc.scalar.copy(zb[:], zt[:].rearrange("c (u e) m -> c u m e", e=2))
+                    zw = right_psum.tile([P, 2, P], F32, name="work")
+                    words = zb[:].rearrange("c u m e -> c (u m e)").bitcast(F32)
+                    for u in range(2):
+                        nc.tensor.transpose(zw[:, u, :], words[:, u * P : (u + 1) * P], ident[:])
+                    nc.scalar.copy(
+                        z_in[:, blk, :].rearrange("p c t -> p (c t)").bitcast(F32).rearrange("p (c u) -> p c u", u=2),
+                        zw[:].rearrange("p u c -> p c u"),
+                    )
             else:
-                nc.vector.tensor_tensor(
-                    z_in[:].rearrange("p (c i) t -> p c t i", i=4),
-                    own[:].rearrange("p t (c i) -> p c t i", i=4),
-                    far[:].rearrange("p t (c i) -> p c t i", i=4),
-                    ALU.add,
-                )
-            quantise(j, z_in)
-            if 1 <= j < BLOCKS - 1:
-                multiply(j - 1)
+                z_sum = keep.tile([P, PACK, n], F32, name="z_sum")
+                nc.vector.tensor_tensor(z_sum[:], own[:], far[:], ALU.add)
+                nc.vector.tensor_copy(z_in[:].rearrange("p (c i) t -> p c t i", i=4), z_sum[:].rearrange("p t (c i) -> p c t i", i=4))
+            nc.vector.quantize_mx(z_codes[:, cols].bitcast(FP8X4), z_scales[:, cols], z_in[:].rearrange("p c t -> p (c t)"))
+            if 1 <= i < len(Z_PIECES) - 1:
+                multiply(slice(Z_PIECES[i - 1][0], start))
         before = slice(S - 2 * P, S - P)
         final = slice(S - P, S)
         both = slice(S - 2 * P, S)
@@ -236,66 +223,52 @@ def tile_picked_twqflowbstd_none_po_kernel(
         out_words = out_1[0].rearrange("p c r -> p (c r)").bitcast(I32)
         o_codes = keep.tile([P, S], I32, name="o_codes", align_bytes=64)
         o_scales = keep.tile([P, S], U8, name="o_scales", align_bytes=64)
-        for start, n in PIECES:
+        res = dict((start, keep.tile([P, PACK, n], F32, name="res%d" % start)) for start, n in PIECES)
+        for start, n, t0, nt, on_pe, held in UNITS:
             cols = slice(start, start + n)
-            res = keep.tile([P, PACK, n], F32, name="res%d" % start)
-            for t0 in range(0, PACK, 2):
-                pair = (t0, t0 + 1)
-                q = dict((t, ring.tile([P, n], F32, name="q", bufs=4)) for t in pair)
-                r = dict((t, ring.tile([P, n], F32, name="r", bufs=4)) for t in pair)
-                num = dict((t, ring.tile([P, n], F32, name="num", bufs=4)) for t in pair)
-                for t in pair:
-                    nc.vector.tensor_tensor(q[t][:], h_win[t][:].indirect(entries(n4_l, start, n)), h_x[t][:, cols], ALU.add)
-                for t in pair:
-                    nc.vector.tensor_tensor(r[t][:], h_win[t][:].indirect(entries(n5_l, start, n)), q[t][:], ALU.subtract)
-                for t in pair:
-                    nc.vector.scalar_tensor_tensor(num[t][:], q[t][:], 2.0, r[t][:], ALU.mult, ALU.add)
-                if start + n < S:
-                    for t in pair:
-                        lin = rows_psum.tile([P, 2, n], F32, name="rows")
+            ts = range(t0, t0 + nt)
+            q = ring.tile([P, nt, n], F32, name="q", bufs=QB)
+            r = ring.tile([P, nt, n], F32, name="held" if held else "r", bufs=NB)
+            num = ring.tile([P, nt, n], F32, name="held" if held else "num", bufs=NB)
+            for t in ts:
+                nc.vector.tensor_tensor(q[:, t - t0, :], h_win[t][:].indirect(entries(n4_l, start, n)), h_x[:, t, cols], ALU.add)
+            for t in ts:
+                nc.vector.tensor_tensor(r[:, t - t0, :], h_win[t][:].indirect(entries(n5_l, start, n)), q[:, t - t0, :], ALU.subtract)
+            nc.vector.scalar_tensor_tensor(num[:], q[:], 2.0, r[:], ALU.mult, ALU.add)
+            sq = ring.tile([P, 2, nt, n], F32, name="sq")
+            inv = ring.tile([P, nt, n], F32, name="inv")
+            for form, (plain, made, factor) in enumerate(((h_x, r, 0.5**0.5), (h_k, num, 0.375 * 0.5**0.5))):
+                if on_pe:
+                    lin = right_psum.tile([P, nt, n], F32, name="work") if LIN == 3 else rows_psum.tile([P, nt, n], F32, name="rows")
+                    for t in ts:
                         for j in range(n // P):
                             blk = slice(j * P, (j + 1) * P)
-                            src = slice(start + j * P, start + (j + 1) * P)
-                            add_transposed(lin[:, 0, blk], [h_x[t][:, src], r[t][:, blk]])
-                        for j in range(n // P):
-                            blk = slice(j * P, (j + 1) * P)
-                            src = slice(start + j * P, start + (j + 1) * P)
-                            add_transposed(lin[:, 1, blk], [h_k[t][:, src], num[t][:, blk]])
-                        sq = ring.tile([P, 2, n], F32, name="sq")
-                        nc.scalar.activation(sq[:, 0, :], lin[:, 0, :], ACT.Square, scale=0.5**0.5)
-                        nc.scalar.activation(sq[:, 1, :], lin[:, 1, :], ACT.Square, scale=0.375 * 0.5**0.5)
-                        tot = right_psum.tile([P, n], F32, name="work")
-                        for j in range(n // P):
-                            blk = slice(j * P, (j + 1) * P)
-                            add_transposed(tot[:, blk], [sq[:, 0, blk], sq[:, 1, blk]])
-                        inv = ring.tile([P, n], F32, name="inv")
-                        nc.scalar.activation(inv[:], tot[:], ACT.Abs_reciprocal_sqrt, bias=quarter[:])
-                        nc.vector.scalar_tensor_tensor(res[:, t, :], num[t][:], -0.3125, inv[:], ALU.mult, ALU.mult)
+                            add_transposed(lin[:, t - t0, blk], [plain[:, t, start + j * P : start + (j + 1) * P], made[:, t - t0, blk]])
                 else:
-                    lin = dict((t, ring.tile([P, 2, n], F32, name="lin", bufs=4)) for t in pair)
-                    sq = dict((t, ring.tile([P, 2, n], F32, name="sq2", bufs=4)) for t in pair)
-                    tot = dict((t, ring.tile([P, n], F32, name="tot", bufs=4)) for t in pair)
-                    inv = dict((t, ring.tile([P, n], F32, name="inv2", bufs=4)) for t in pair)
-                    for t in pair:
-                        nc.vector.tensor_tensor(lin[t][:, 0, :], r[t][:], h_x[t][:, cols], ALU.add)
-                        nc.scalar.activation(sq[t][:, 0, :], lin[t][:, 0, :], ACT.Square, scale=0.5**0.5)
-                    for t in pair:
-                        nc.vector.tensor_tensor(lin[t][:, 1, :], num[t][:], h_k[t][:, cols], ALU.add)
-                        nc.scalar.activation(sq[t][:, 1, :], lin[t][:, 1, :], ACT.Square, scale=0.375 * 0.5**0.5)
-                    for t in pair:
-                        nc.vector.tensor_tensor(tot[t][:], sq[t][:, 0, :], sq[t][:, 1, :], ALU.add)
-                        nc.scalar.activation(inv[t][:], tot[t][:], ACT.Abs_reciprocal_sqrt, bias=quarter[:])
-                    for t in pair:
-                        nc.vector.scalar_tensor_tensor(res[:, t, :], num[t][:], -0.3125, inv[t][:], ALU.mult, ALU.mult)
-            nc.sync.dma_start(out_rows[:, :, cols], res[:])
-            o_in = keep.tile([P, n, PACK], BF16, name="o_in%d" % start, align_bytes=64)
-            dst = o_in[:].rearrange("p (c i) t -> p c t i", i=4)
-            src = res[:].rearrange("p t (c i) -> p c t i", i=4)
-            if start + n < S:
-                nc.scalar.copy(dst, src)
+                    lin = ring.tile([P, nt, n], F32, name="lin", bufs=4)
+                    nc.vector.tensor_tensor(lin[:], made[:], plain[:, t0 : t0 + nt, cols], ALU.add)
+                nc.scalar.activation(sq[:, form], lin[:], ACT.Square, scale=factor)
+            if on_pe:
+                tot = rows_psum.tile([P, nt, n], F32, name="rows") if LIN == 3 else right_psum.tile([P, nt, n], F32, name="work")
+                for t in ts:
+                    for j in range(n // P):
+                        blk = slice(j * P, (j + 1) * P)
+                        add_transposed(tot[:, t - t0, blk], [sq[:, 0, t - t0, blk], sq[:, 1, t - t0, blk]])
             else:
-                nc.vector.tensor_copy(dst, src)
-            nc.vector.quantize_mx(o_codes[:, cols].bitcast(FP8X4), o_scales[:, cols], o_in[:].rearrange("p c t -> p (c t)"))
-            nc.sync.dma_start(out_words[:, cols], o_codes[:, cols])
+                tot = ring.tile([P, nt, n], F32, name="tot")
+                nc.vector.tensor_tensor(tot[:], sq[:, 0], sq[:, 1], ALU.add)
+            nc.scalar.activation(inv[:], tot[:], ACT.Abs_reciprocal_sqrt, bias=quarter[:])
+            nc.vector.scalar_tensor_tensor(res[start][:, t0 : t0 + nt, :], num[:], -0.3125, inv[:], ALU.mult, ALU.mult)
+            if t0 + nt == PACK:
+                nc.sync.dma_start(out_rows[:, :, cols], res[start][:])
+                o_in = keep.tile([P, n, PACK], BF16, name="o_in%d" % start, align_bytes=64)
+                dst = o_in[:].rearrange("p (c i) t -> p c t i", i=4)
+                src = res[start][:].rearrange("p t (c i) -> p c t i", i=4)
+                if start < ILV:
+                    nc.scalar.copy(dst, src)
+                else:
+                    nc.vector.tensor_copy(dst, src)
+                nc.vector.quantize_mx(o_codes[:, cols].bitcast(FP8X4), o_scales[:, cols], o_in[:].rearrange("p c t -> p (c t)"))
+                nc.sync.dma_start(out_words[:, cols], o_codes[:, cols])
         for quad in range(4):
             nc.sync.dma_start(out_2[0].bitcast(I32)[4 * quad : 4 * quad + 4, :], o_scales[32 * quad : 32 * quad + 4, :].bitcast(I32))

@@ -18,12 +18,18 @@ ALU = mybir.AluOpType
 ACT = mybir.ActivationFunctionType
 
 P = 128
-PACK = 4
-BLOCKS = S // P
+SLOTS = 4
+PER_COLUMN = 16
+QUADRANT = 32
 PIECES = ((0, 256), (256, 128), (384, 128))
-Z_PIECES = ((0, 256), (256, 128), (384, 128))
-UNITS = ((0, 256, 0, 2, True, False), (0, 256, 2, 2, True, False), (256, 128, 0, 4, True, False), (384, 128, 0, 3, True, False), (384, 128, 3, 1, True, False))
-QB, NB, YS, ILV, LIN = 2, 3, 4, 0, 4
+STEPS = ((0, 256, 0, 2), (0, 256, 2, 2), (256, 128, 0, 4), (384, 128, 0, 2), (384, 128, 2, 2))
+
+H_SCALE = 0.0625
+MU_SCALE = 0.3125
+H_IN_SPREAD = -5.0 / 3.0
+SPREAD_TO_CENTRED = (11.0 / 5.0) / (5.0 / 3.0)
+GAP_SCALE = 0.5**0.5
+SPREAD_SCALE = 0.375 * 0.5**0.5
 
 
 def tile_picked_twqflowbstd_none_po_kernel(
@@ -34,61 +40,71 @@ def tile_picked_twqflowbstd_none_po_kernel(
     with ExitStack() as ctx:
         keep = ctx.enter_context(tc.tile_pool(name="keep", bufs=1))
         ring = ctx.enter_context(tc.tile_pool(name="ring", bufs=3))
-        rows_psum = ctx.enter_context(tc.psum_pool(name="rows_psum", bufs=4))
-        left_psum = ctx.enter_context(tc.psum_pool(name="left_psum", bufs=1))
-        right_psum = ctx.enter_context(tc.psum_pool(name="right_psum", bufs=3))
+        slot_psum = ctx.enter_context(tc.psum_pool(name="slot_psum", bufs=SLOTS))
+        first_psum = ctx.enter_context(tc.psum_pool(name="first_psum", bufs=1))
+        work_psum = ctx.enter_context(tc.psum_pool(name="work_psum", bufs=3))
 
         def load_list(name, src):
-            tile = keep.tile([P, S // 16], U16, name=name)
+            tile = keep.tile([P, S // PER_COLUMN], U16, name=name)
             nc.sync.dma_start(tile[:], src)
             return tile
 
         def entries(lst, start, n):
-            return lst[:, start // 16 : (start + n) // 16]
+            return lst[:, start // PER_COLUMN : (start + n) // PER_COLUMN]
 
-        def zeroed_plane(name, width, engine):
+        def zeroed_scales(name, width, engine):
             tile = keep.tile([P, width], U8, name=name, align_bytes=64)
             engine.memset(tile[:].bitcast(I32), 0)
             return tile
 
-        def load_plane(tile, scales, places, engines):
+        def load_scales(tile, scales, places):
             rows = scales[0].bitcast(I32).rearrange("(q r) c -> r q c", r=4)
-            for r in range(4):
-                engines[r].dma_start(tile[places[r] : P : 32, :].bitcast(I32), rows[r])
+            for r, place in enumerate(places):
+                nc.sync.dma_start(tile[place:P:QUADRANT, :].bitcast(I32), rows[r])
+
+        def load_words(name, words, width):
+            tile = keep.tile([P, width], I32, name=name)
+            nc.sync.dma_start(tile[:], words[0].rearrange("p c r -> p (c r)").bitcast(I32))
+            return tile
+
+        def load_fp4(name, words):
+            tile = keep.tile([P, 2 * H], U8, name=name, align_bytes=64)
+            nc.sync.dma_start(tile[:].bitcast(I32), words[0].bitcast(I32))
+            return tile
 
         def add_transposed(out, parts):
             for i, part in enumerate(parts):
                 nc.tensor.matmul(out, part, ident[:], is_transpose=True, start=(i == 0), stop=(i == len(parts) - 1))
 
-        xs = zeroed_plane("xs", T, nc.gpsimd)
-        w1s = zeroed_plane("w1s", H, nc.vector)
-        ds = zeroed_plane("ds", G, nc.vector)
-        w2s = zeroed_plane("w2s", H, nc.vector)
-        dk_scales = zeroed_plane("dk_scales", H, nc.vector)
-        on_sync = (nc.sync,) * 4
+        def side_by_side(engine_copy, dst, src):
+            engine_copy(dst.rearrange("p (c i) t -> p c t i", i=4), src.rearrange("p t (c i) -> p c t i", i=4))
 
-        offs_l = load_list("offs_l", offs)
-        xw = keep.tile([P, T], I32, name="xw")
-        nc.sync.dma_start(xw[:], x_words[0].rearrange("p c r -> p (c r)").bitcast(I32))
-        load_plane(xs, x_scales, (0, 1, 2, 3), on_sync)
-        w1w = keep.tile([P, 2 * H], U8, name="w1w", align_bytes=64)
-        nc.sync.dma_start(w1w[:].bitcast(I32), w1_words[0].bitcast(I32))
-        two_l = load_list("two_l", two)
-        load_plane(w1s, w1_scales, (0, 1, 2, 3), on_sync)
-        k1_l = load_list("k1_l", k1)
-        dw = keep.tile([P, G], I32, name="dw")
-        nc.sync.dma_start(dw[:], d_words[0].rearrange("p c r -> p (c r)").bitcast(I32))
-        load_plane(ds, d_scales, (0, 1, 16, 17), on_sync)
-        w2w = keep.tile([P, 2 * H], U8, name="w2w", align_bytes=64)
-        nc.sync.dma_start(w2w[:].bitcast(I32), w2_words[0].bitcast(I32))
-        load_plane(w2s, w2_scales, (0, 1, 2, 3), on_sync)
-        n2_l = load_list("n2_l", n2)
-        n1_l = load_list("n1_l", n1)
-        gs_t = keep.tile([P, PACK], F32, name="gs_t")
-        nc.sync.dma_start(gs_t[:], gs.rearrange("(p t) o -> p (t o)", t=PACK))
-        n3_l = load_list("n3_l", n3)
-        n4_l = load_list("n4_l", n4)
-        n5_l = load_list("n5_l", n5)
+        x_scale_table = zeroed_scales("x_scale_table", T, nc.gpsimd)
+        w1_scale_tile = zeroed_scales("w1_scale_tile", H, nc.vector)
+        d_scale_table = zeroed_scales("d_scale_table", G, nc.vector)
+        w2_scale_tile = zeroed_scales("w2_scale_tile", H, nc.vector)
+        code_scales = zeroed_scales("code_scales", H, nc.vector)
+        in_place = (0, 1, 2, 3)
+        by_run = (0, 1, 16, 17)
+
+        offs_list = load_list("offs_list", offs)
+        x_word_table = load_words("x_word_table", x_words, T)
+        load_scales(x_scale_table, x_scales, in_place)
+        w1_word_tile = load_fp4("w1_word_tile", w1_words)
+        two_list = load_list("two_list", two)
+        load_scales(w1_scale_tile, w1_scales, in_place)
+        k1_list = load_list("k1_list", k1)
+        d_word_table = load_words("d_word_table", d_words, G)
+        load_scales(d_scale_table, d_scales, by_run)
+        w2_word_tile = load_fp4("w2_word_tile", w2_words)
+        load_scales(w2_scale_tile, w2_scales, in_place)
+        n2_list = load_list("n2_list", n2)
+        n1_list = load_list("n1_list", n1)
+        gs_slots = keep.tile([P, SLOTS], F32, name="gs_slots")
+        nc.sync.dma_start(gs_slots[:], gs.rearrange("(p t) o -> p (t o)", t=SLOTS))
+        n3_list = load_list("n3_list", n3)
+        n4_list = load_list("n4_list", n4)
+        n5_list = load_list("n5_list", n5)
 
         sixteen = keep.tile([P, 1], F32, name="sixteen")
         nc.gpsimd.memset(sixteen[:], 16.0)
@@ -96,179 +112,179 @@ def tile_picked_twqflowbstd_none_po_kernel(
         nc.scalar.activation(quarter[:], sixteen[:], ACT.Abs_reciprocal_sqrt)
         ident = keep.tile([P, P], F32, name="ident")
         make_identity(nc, ident[:])
-        y_win = [keep.tile([P, S], F32, name="y_win%d" % t) for t in range(PACK)]
-        half_gs = keep.tile([P, PACK], F32, name="half_gs")
-        nc.gpsimd.tensor_scalar(half_gs[:], gs_t[:], 0.5, 0.0, ALU.mult, ALU.add)
+        y_wide = [keep.tile([P, 2 * S], F32, name="y_wide%d" % t) for t in range(SLOTS)]
+        d_wide = [keep.tile([P, 2 * S], F32, name="d_wide%d" % t) for t in range(SLOTS)]
+        for t in range(SLOTS):
+            nc.vector.memset(y_wide[t][:, S:], 0.0)
+            nc.gpsimd.memset(d_wide[t][:, S:], 0.0)
+        half_gs = keep.tile([P, SLOTS], F32, name="half_gs")
+        nc.gpsimd.tensor_scalar(half_gs[:], gs_slots[:], 0.5, 0.0, ALU.mult, ALU.add)
 
-        def pick(name, words, plane, lst, cuts):
-            pw = keep.tile([P, S], I32, name=name + "_w", align_bytes=64)
-            ps = keep.tile([P, S], U8, name=name + "_s", align_bytes=64)
-            for start, n in cuts:
-                nc.vector.tensor_copy(pw[:, start : start + n].bitcast(U32), words[:].bitcast(U32).indirect(entries(lst, start, n)))
-                nc.vector.tensor_copy(ps[:, start : start + n], plane[:].indirect(entries(lst, start, n)))
-            return pw, ps
+        def pick(name, word_table, scale_table, lst, n):
+            words = keep.tile([P, S], I32, name=name + "_words", align_bytes=64)
+            scales = keep.tile([P, S], U8, name=name + "_scales", align_bytes=64)
+            for start in range(0, S, n):
+                part = entries(lst, start, n)
+                nc.vector.tensor_copy(words[:, start : start + n].bitcast(U32), word_table[:].bitcast(U32).indirect(part))
+                nc.vector.tensor_copy(scales[:, start : start + n], scale_table[:].indirect(part))
+            return words, scales
 
-        xq_w, xq_s = pick("xq", xw, xs, offs_l, ((0, 256), (256, 256)))
-        xt_w, xt_s = pick("xt", xw, xs, two_l, ((0, 512),))
-        dg_w, dg_s = pick("dg", dw, ds, k1_l, ((0, 512),))
-        dk_words = keep.tile([P, H], I32, name="dk_words", align_bytes=64)
-        nc.vector.tensor_copy(dk_words[:].rearrange("p (t m) -> p t m", t=PACK), dg_w[:].rearrange("p (m t) -> p t m", t=PACK))
-        dealt_s = keep.tile([P, H], U8, name="dealt_s")
-        nc.vector.tensor_copy(dealt_s[:].rearrange("p (t m) -> p t m", t=PACK), dg_s[:].rearrange("p (m t) -> p t m", t=PACK))
-        for r, place in enumerate((0, 1, 16, 17)):
-            nc.sync.dma_start(dk_scales[r:P:32, :].bitcast(I32), dealt_s[place:P:32, :].bitcast(I32))
+        y_token_words, y_token_scales = pick("y_token", x_word_table, x_scale_table, offs_list, S // 2)
+        d_token_words, d_token_scales = pick("d_token", x_word_table, x_scale_table, two_list, S)
+        picked_words, picked_scales = pick("picked", d_word_table, d_scale_table, k1_list, S)
+        code_words = keep.tile([P, H], I32, name="code_words", align_bytes=64)
+        nc.vector.tensor_copy(
+            code_words[:].rearrange("p (t m) -> p t m", t=SLOTS), picked_words[:].rearrange("p (m t) -> p t m", t=SLOTS)
+        )
+        dealt_scales = keep.tile([P, H], U8, name="dealt_scales")
+        nc.vector.tensor_copy(
+            dealt_scales[:].rearrange("p (t m) -> p t m", t=SLOTS), picked_scales[:].rearrange("p (m t) -> p t m", t=SLOTS)
+        )
+        for r, place in enumerate(by_run):
+            nc.sync.dma_start(code_scales[r:P:QUADRANT, :].bitcast(I32), dealt_scales[place:P:QUADRANT, :].bitcast(I32))
 
-        def project(name, pw, ps, ww, ws):
-            banks = [rows_psum.tile([P, S], F32, name="rows") for t in range(PACK)]
-            for j in range(BLOCKS):
-                cols = slice(j * P, (j + 1) * P)
-                acc = right_psum.tile([P, H], F32, name="work")
-                nc.tensor.matmul_mx(acc[:], pw[:, cols].bitcast(FP8X4), ps[:, cols], ww[:].bitcast(FP4X4), ws[:], start=True, stop=True)
-                turned = ring.tile([P, PACK, P], F32, name="turned")
-                nc.scalar.copy(turned[:], acc[:].rearrange("p (m t) -> p t m", t=PACK))
-                for t in range(PACK):
-                    nc.tensor.transpose(banks[t][:, cols], turned[:, t, :], ident[:])
+        def project(token_words, token_scales, w_words, w_scales):
+            banks = [slot_psum.tile([P, S], F32, name="slot_bank") for t in range(SLOTS)]
+            for start in range(0, S, P):
+                tokens = slice(start, start + P)
+                by_token = work_psum.tile([P, H], F32, name="work_bank")
+                nc.tensor.matmul_mx(
+                    by_token[:], token_words[:, tokens].bitcast(FP8X4), token_scales[:, tokens],
+                    w_words[:].bitcast(FP4X4), w_scales[:], start=True, stop=True,
+                )
+                sorted_by_slot = ring.tile([P, SLOTS, P], F32, name="sorted_by_slot")
+                nc.scalar.copy(sorted_by_slot[:], by_token[:].rearrange("c (m t) -> c t m", t=SLOTS))
+                for t in range(SLOTS):
+                    nc.tensor.transpose(banks[t][:, tokens], sorted_by_slot[:, t, :], ident[:])
             return banks
 
-        y_banks = project("y", xq_w, xq_s, w1w, w1s)
-        y_plain = [keep.tile([P, S], F32, name="y_plain%d" % t) for t in range(PACK)]
-        for t in range(PACK):
-            nc.scalar.copy(y_win[t][:, :S], y_banks[t][:])
-            if t < YS:
-                nc.scalar.copy(y_plain[t][:], y_banks[t][:])
-            else:
-                nc.sync.dma_start(y_plain[t][:], y_win[t][:, :S])
-        d_banks = project("d", xt_w, xt_s, w2w, w2s)
-        d_win = [keep.tile([P, S], F32, name="d_win%d" % t) for t in range(PACK)]
-        for t in range(PACK):
-            nc.scalar.activation(d_win[t][:], d_banks[t][:], ACT.Copy, scale=half_gs[:, t : t + 1])
+        y_banks = project(y_token_words, y_token_scales, w1_word_tile, w1_scale_tile)
+        y_narrow = [keep.tile([P, S], F32, name="y_narrow%d" % t) for t in range(SLOTS)]
+        for t in range(SLOTS):
+            nc.scalar.copy(y_wide[t][:, :S], y_banks[t][:])
+            nc.scalar.copy(y_narrow[t][:], y_banks[t][:])
+        d_banks = project(d_token_words, d_token_scales, w2_word_tile, w2_scale_tile)
+        for t in range(SLOTS):
+            nc.scalar.activation(d_wide[t][:, :S], d_banks[t][:], ACT.Copy, scale=half_gs[:, t : t + 1])
 
+        diff2 = keep.tile([P, SLOTS, S], F32, name="diff2")
+        far = keep.tile([P, SLOTS, S], F32, name="far")
+        for t in range(SLOTS):
+            nc.vector.tensor_tensor(diff2[:, t, :], y_wide[t][:].indirect(n2_list[:]), y_narrow[t][:], ALU.subtract)
 
         z_codes = keep.tile([P, S], U32, name="z_codes", align_bytes=64)
         z_scales = keep.tile([P, S], U8, name="z_scales", align_bytes=64)
-        h_banks = [rows_psum.tile([P, S], F32, name="rows") for t in range(PACK)]
-        h_win = [keep.tile([P, S], F32, name="h_win%d" % t) for t in range(PACK)]
-        h_x = keep.tile([P, PACK, S], F32, name="h_x")
-        h_k = keep.tile([P, PACK, S], F32, name="h_k")
+        h_banks = [slot_psum.tile([P, S], F32, name="slot_bank") for t in range(SLOTS)]
+        h = [keep.tile([P, S], F32, name="h%d" % t) for t in range(SLOTS)]
 
-        def product(cols, t):
-            m = slice(t * P, (t + 1) * P)
-            nc.tensor.matmul_mx(h_banks[t][:, cols], dk_words[:, m].bitcast(FP8X4), dk_scales[:, m], z_codes[:, cols].bitcast(FP8X4), z_scales[:, cols], start=True, stop=True)
-
-        def scaled(dst, cols, t, factor):
-            nc.scalar.activation(dst[t][:, cols] if isinstance(dst, list) else dst[:, t, cols], h_banks[t][:, cols], ACT.Copy, scale=factor * 0.0625)
-
-        def multiply(cols):
-            for t in range(PACK):
-                product(cols, t)
-            for t in range(PACK):
-                scaled(h_win, cols, t, 1.0)
-                scaled(h_x, cols, t, -2.2)
-                scaled(h_k, cols, t, 8.0 / 15.0)
-
-        for i, (start, n) in enumerate(Z_PIECES):
+        def make_h(start, n):
             cols = slice(start, start + n)
-            last = start + n == S
-            diffs = keep.tile([P, 2, PACK, n], F32, name="z_in0" if last else "diffs", align_bytes=64)
-            diff1 = [diffs[:, 0, t, :] for t in range(PACK)]
-            own = keep.tile([P, PACK, n], F32, name="own%d" % i)
-            z_in = keep.tile([P, n, PACK], BF16, name="z_in%d" % i, align_bytes=64)
-            far = keep.tile([P, PACK, n], F32, name="z_in1" if last else "far%d" % i, align_bytes=64)
-            diff2 = [diffs[:, 1, t, :] for t in range(PACK)]
-            for t in range(PACK):
-                nc.vector.tensor_tensor(diff2[t][:], y_win[t][:].indirect(entries(n2_l, start, n)), y_plain[t][:, cols], ALU.subtract)
-                nc.vector.tensor_tensor(diff1[t][:], y_win[t][:].indirect(entries(n1_l, start, n)), y_plain[t][:, cols], ALU.subtract)
-            for step in (0, 1):
-                for t in range(PACK):
-                    if step == 0:
-                        nc.vector.scalar_tensor_tensor(own[:, t, :], diff1[t][:], 2.0, d_win[t][:, cols], ALU.mult, ALU.mult)
-                    else:
-                        nc.vector.tensor_tensor(far[:, t, :], d_win[t][:].indirect(entries(n3_l, start, n)), diff2[t][:], ALU.mult)
-            if not last:
+            for t in range(SLOTS):
+                features = slice(t * P, (t + 1) * P)
+                nc.tensor.matmul_mx(
+                    h_banks[t][:, cols], code_words[:, features].bitcast(FP8X4), code_scales[:, features],
+                    z_codes[:, cols].bitcast(FP8X4), z_scales[:, cols], start=True, stop=True,
+                )
+            for t in range(SLOTS):
+                nc.scalar.activation(h[t][:, cols], h_banks[t][:, cols], ACT.Copy, scale=H_SCALE)
+
+        def add_and_round_turned(z_bf16, own, start, j):
+            block = slice(j * P, (j + 1) * P)
+            pool, name = (first_psum, "first_bank") if j == 0 else (work_psum, "work_bank")
+            z_turned = pool.tile([P, SLOTS, P], F32, name=name)
+            for t in range(SLOTS):
+                add_transposed(z_turned[:, t, :], [far[:, t, start + j * P : start + (j + 1) * P], own[:, t, block]])
+            pairs = ring.tile([P, 2, P, 2], BF16, name="pairs")
+            nc.scalar.copy(pairs[:], z_turned[:].rearrange("c (u e) p -> c u p e", e=2))
+            pair_words = pairs[:].rearrange("c u p e -> c (u p e)").bitcast(F32)
+            pairs_back = work_psum.tile([P, 2, P], F32, name="work_bank")
+            for u in range(2):
+                nc.tensor.transpose(pairs_back[:, u, :], pair_words[:, u * P : (u + 1) * P], ident[:])
+            nc.scalar.copy(
+                z_bf16[:, block, :].rearrange("p c t -> p (c t)").bitcast(F32).rearrange("p (c u) -> p c u", u=2),
+                pairs_back[:].rearrange("p u c -> p c u"),
+            )
+
+        for i, (start, n) in enumerate(PIECES):
+            cols = slice(start, start + n)
+            last = i == len(PIECES) - 1
+            diff1 = keep.tile([P, SLOTS, n], F32, name="diff1", align_bytes=64)
+            own = keep.tile([P, SLOTS, n], F32, name="z_bf16_0" if last else "own%d" % i, align_bytes=64)
+            z_bf16 = keep.tile([P, n, SLOTS], BF16, name="z_bf16_%d" % i, align_bytes=64)
+            for t in range(SLOTS):
+                nc.vector.tensor_tensor(
+                    diff1[:, t, :], y_narrow[t][:].indirect(entries(n1_list, start, n)), y_wide[t][:, cols], ALU.subtract
+                )
+            if i == 0:
+                for t in range(SLOTS):
+                    nc.vector.tensor_tensor(far[:, t, :], d_wide[t][:].indirect(n3_list[:]), diff2[:, t, :], ALU.mult)
+            for t in range(SLOTS):
+                nc.vector.scalar_tensor_tensor(own[:, t, :], diff1[:, t, :], 2.0, d_wide[t][:, cols], ALU.mult, ALU.mult)
+            if last:
+                z_last = keep.tile([P, SLOTS, n], F32, name="z_last")
+                nc.vector.tensor_tensor(z_last[:], own[:], far[:, :, cols], ALU.add)
+                side_by_side(nc.vector.tensor_copy, z_bf16[:], z_last[:])
+            else:
                 for j in range(n // P):
-                    blk = slice(j * P, (j + 1) * P)
-                    zt = left_psum.tile([P, PACK, P], F32, name="zt", bufs=1)
-                    for t in range(PACK):
-                        add_transposed(zt[:, t, :], [own[:, t, blk], far[:, t, blk]])
-                    zb = ring.tile([P, 2, P, 2], BF16, name="zb")
-                    nc.scalar.copy(zb[:], zt[:].rearrange("c (u e) m -> c u m e", e=2))
-                    zw = right_psum.tile([P, 2, P], F32, name="work")
-                    words = zb[:].rearrange("c u m e -> c (u m e)").bitcast(F32)
-                    for u in range(2):
-                        nc.tensor.transpose(zw[:, u, :], words[:, u * P : (u + 1) * P], ident[:])
-                    nc.scalar.copy(
-                        z_in[:, blk, :].rearrange("p c t -> p (c t)").bitcast(F32).rearrange("p (c u) -> p c u", u=2),
-                        zw[:].rearrange("p u c -> p c u"),
-                    )
-            else:
-                z_sum = keep.tile([P, PACK, n], F32, name="z_sum")
-                nc.vector.tensor_tensor(z_sum[:], own[:], far[:], ALU.add)
-                nc.vector.tensor_copy(z_in[:].rearrange("p (c i) t -> p c t i", i=4), z_sum[:].rearrange("p t (c i) -> p c t i", i=4))
-            nc.vector.quantize_mx(z_codes[:, cols].bitcast(FP8X4), z_scales[:, cols], z_in[:].rearrange("p c t -> p (c t)"))
-            if 1 <= i < len(Z_PIECES) - 1:
-                multiply(slice(Z_PIECES[i - 1][0], start))
-        before = slice(S - 2 * P, S - P)
-        final = slice(S - P, S)
-        both = slice(S - 2 * P, S)
-        for cols in (before, final):
-            for t in range(PACK):
-                product(cols, t)
-            for t in range(PACK):
-                scaled(h_win, cols, t, 1.0)
-                scaled(h_x, cols, t, -2.2)
-        for t in range(PACK):
-            scaled(h_k, both, t, 8.0 / 15.0)
+                    add_and_round_turned(z_bf16, own, start, j)
+            nc.vector.quantize_mx(z_codes[:, cols].bitcast(FP8X4), z_scales[:, cols], z_bf16[:].rearrange("p c t -> p (c t)"))
+            if i > 0:
+                make_h(*PIECES[i - 1])
+        make_h(*PIECES[-1])
+        h_part = keep.tile([P, SLOTS, S], F32, name="h_part")
+        for t in range(SLOTS):
+            nc.scalar.activation(h_part[:, t, :], h_banks[t][:], ACT.Copy, scale=H_IN_SPREAD * H_SCALE)
 
-        out_rows = out_0.rearrange("(p t) c -> p t c", t=PACK)
+        out_slots = out_0.rearrange("(p t) c -> p t c", t=SLOTS)
         out_words = out_1[0].rearrange("p c r -> p (c r)").bitcast(I32)
-        o_codes = keep.tile([P, S], I32, name="o_codes", align_bytes=64)
-        o_scales = keep.tile([P, S], U8, name="o_scales", align_bytes=64)
-        res = dict((start, keep.tile([P, PACK, n], F32, name="res%d" % start)) for start, n in PIECES)
-        for start, n, t0, nt, on_pe, held in UNITS:
+        out_codes = keep.tile([P, S], I32, name="out_codes", align_bytes=64)
+        out_scales = keep.tile([P, S], U8, name="out_scales", align_bytes=64)
+        result = dict((start, keep.tile([P, SLOTS, n], F32, name="result%d" % start)) for start, n in PIECES)
+        for start, n, t0, count in STEPS:
             cols = slice(start, start + n)
-            ts = range(t0, t0 + nt)
-            q = ring.tile([P, nt, n], F32, name="q", bufs=QB)
-            r = ring.tile([P, nt, n], F32, name="held" if held else "r", bufs=NB)
-            num = ring.tile([P, nt, n], F32, name="held" if held else "num", bufs=NB)
-            for t in ts:
-                nc.vector.tensor_tensor(q[:, t - t0, :], h_win[t][:].indirect(entries(n4_l, start, n)), h_x[:, t, cols], ALU.add)
-            for t in ts:
-                nc.vector.tensor_tensor(r[:, t - t0, :], h_win[t][:].indirect(entries(n5_l, start, n)), q[:, t - t0, :], ALU.subtract)
-            nc.vector.scalar_tensor_tensor(num[:], q[:], 2.0, r[:], ALU.mult, ALU.add)
-            sq = ring.tile([P, 2, nt, n], F32, name="sq")
-            inv = ring.tile([P, nt, n], F32, name="inv")
-            for form, (plain, made, factor) in enumerate(((h_x, r, 0.5**0.5), (h_k, num, 0.375 * 0.5**0.5))):
-                if on_pe:
-                    lin = right_psum.tile([P, nt, n], F32, name="work") if LIN == 3 else rows_psum.tile([P, nt, n], F32, name="rows")
-                    for t in ts:
-                        for j in range(n // P):
-                            blk = slice(j * P, (j + 1) * P)
-                            add_transposed(lin[:, t - t0, blk], [plain[:, t, start + j * P : start + (j + 1) * P], made[:, t - t0, blk]])
-                else:
-                    lin = ring.tile([P, nt, n], F32, name="lin", bufs=4)
-                    nc.vector.tensor_tensor(lin[:], made[:], plain[:, t0 : t0 + nt, cols], ALU.add)
-                nc.scalar.activation(sq[:, form], lin[:], ACT.Square, scale=factor)
-            if on_pe:
-                tot = rows_psum.tile([P, nt, n], F32, name="rows") if LIN == 3 else right_psum.tile([P, nt, n], F32, name="work")
-                for t in ts:
-                    for j in range(n // P):
-                        blk = slice(j * P, (j + 1) * P)
-                        add_transposed(tot[:, t - t0, blk], [sq[:, 0, t - t0, blk], sq[:, 1, t - t0, blk]])
-            else:
-                tot = ring.tile([P, nt, n], F32, name="tot")
-                nc.vector.tensor_tensor(tot[:], sq[:, 0], sq[:, 1], ALU.add)
-            nc.scalar.activation(inv[:], tot[:], ACT.Abs_reciprocal_sqrt, bias=quarter[:])
-            nc.vector.scalar_tensor_tensor(res[start][:, t0 : t0 + nt, :], num[:], -0.3125, inv[:], ALU.mult, ALU.mult)
-            if t0 + nt == PACK:
-                nc.sync.dma_start(out_rows[:, :, cols], res[start][:])
-                o_in = keep.tile([P, n, PACK], BF16, name="o_in%d" % start, align_bytes=64)
-                dst = o_in[:].rearrange("p (c i) t -> p c t i", i=4)
-                src = res[start][:].rearrange("p t (c i) -> p c t i", i=4)
-                if start < ILV:
-                    nc.scalar.copy(dst, src)
-                else:
-                    nc.vector.tensor_copy(dst, src)
-                nc.vector.quantize_mx(o_codes[:, cols].bitcast(FP8X4), o_scales[:, cols], o_in[:].rearrange("p c t -> p (c t)"))
-                nc.sync.dma_start(out_words[:, cols], o_codes[:, cols])
-        for quad in range(4):
-            nc.sync.dma_start(out_2[0].bitcast(I32)[4 * quad : 4 * quad + 4, :], o_scales[32 * quad : 32 * quad + 4, :].bitcast(I32))
+            slots = slice(t0, t0 + count)
+            blocks = [(a, j * P) for a in range(count) for j in range(n // P)]
+            pa = ring.tile([P, count, n], F32, name="pa", bufs=2)
+            gap = ring.tile([P, count, n], F32, name="gap")
+            both = ring.tile([P, count, n], F32, name="both")
+            centred = ring.tile([P, count, n], F32, name="centred")
+            for a in range(count):
+                nc.vector.tensor_copy(pa[:, a, :], h[t0 + a][:].indirect(entries(n4_list, start, n)))
+            for a in range(count):
+                nc.vector.tensor_tensor(both[:, a, :], h[t0 + a][:].indirect(entries(n5_list, start, n)), pa[:, a, :], ALU.add)
+            nc.vector.scalar_tensor_tensor(gap[:], pa[:], 2.0, both[:], ALU.mult, ALU.subtract)
+            nc.vector.scalar_tensor_tensor(centred[:], h_part[:, slots, cols], SPREAD_TO_CENTRED, both[:], ALU.mult, ALU.add)
+
+            squares = ring.tile([P, 2, count, n], F32, name="squares")
+            inverse_root = ring.tile([P, count, n], F32, name="inverse_root")
+            spread_turned = slot_psum.tile([P, count, n], F32, name="slot_bank")
+            for a, c in blocks:
+                add_transposed(
+                    spread_turned[:, a, c : c + P], [h_part[:, t0 + a, start + c : start + c + P], both[:, a, c : c + P]]
+                )
+            nc.scalar.activation(squares[:, 1], spread_turned[:], ACT.Square, scale=SPREAD_SCALE)
+            gap_turned = slot_psum.tile([P, count, n], F32, name="slot_bank")
+            for a, c in blocks:
+                add_transposed(gap_turned[:, a, c : c + P], [gap[:, a, c : c + P]])
+            nc.scalar.activation(squares[:, 0], gap_turned[:], ACT.Square, scale=GAP_SCALE)
+            total = work_psum.tile([P, count, n], F32, name="work_bank")
+            for a, c in blocks:
+                add_transposed(total[:, a, c : c + P], [squares[:, 1, a, c : c + P], squares[:, 0, a, c : c + P]])
+            nc.scalar.activation(inverse_root[:], total[:], ACT.Abs_reciprocal_sqrt, bias=quarter[:])
+            nc.vector.scalar_tensor_tensor(
+                result[start][:, slots, :], centred[:], -MU_SCALE, inverse_root[:], ALU.mult, ALU.mult
+            )
+
+            if t0 + count == SLOTS:
+                nc.sync.dma_start(out_slots[:, :, cols], result[start][:])
+                out_bf16 = keep.tile([P, n, SLOTS], BF16, name="out_bf16_%d" % start, align_bytes=64)
+                side_by_side(nc.scalar.copy if start == 0 else nc.vector.tensor_copy, out_bf16[:], result[start][:])
+                nc.vector.quantize_mx(
+                    out_codes[:, cols].bitcast(FP8X4), out_scales[:, cols], out_bf16[:].rearrange("p c t -> p (c t)")
+                )
+                nc.sync.dma_start(out_words[:, cols], out_codes[:, cols])
+        for quad in range(P // QUADRANT):
+            nc.sync.dma_start(
+                out_2[0].bitcast(I32)[4 * quad : 4 * quad + 4, :],
+                out_scales[QUADRANT * quad : QUADRANT * quad + 4, :].bitcast(I32),
+            )

@@ -23,11 +23,12 @@ PER_COLUMN = 16
 QUADRANT = 32
 PIECES = ((0, 256), (256, 128), (384, 128))
 STEPS = ((0, 256, 0, 2), (0, 256, 2, 2), (256, 128, 0, 4), (384, 128, 0, 2), (384, 128, 2, 2))
+LAST_START, LAST_WIDTH = PIECES[-1]
 
 H_SCALE = 0.0625
 MU_SCALE = 0.3125
+H_IN_CENTRED = -11.0 / 5.0
 H_IN_SPREAD = -5.0 / 3.0
-SPREAD_TO_CENTRED = (11.0 / 5.0) / (5.0 / 3.0)
 GAP_SCALE = 0.5**0.5
 SPREAD_SCALE = 0.375 * 0.5**0.5
 
@@ -76,8 +77,11 @@ def tile_picked_twqflowbstd_none_po_kernel(
             for i, part in enumerate(parts):
                 nc.tensor.matmul(out, part, ident[:], is_transpose=True, start=(i == 0), stop=(i == len(parts) - 1))
 
-        def side_by_side(engine_copy, dst, src):
-            engine_copy(dst.rearrange("p (c i) t -> p c t i", i=4), src.rearrange("p t (c i) -> p c t i", i=4))
+        def as_columns(tile):
+            return tile.rearrange("p (c i) t -> p c t i", i=4)
+
+        def as_slots(tile):
+            return tile.rearrange("p t (c i) -> p c t i", i=4)
 
         x_scale_table = zeroed_scales("x_scale_table", T, nc.gpsimd)
         w1_scale_tile = zeroed_scales("w1_scale_tile", H, nc.vector)
@@ -112,11 +116,6 @@ def tile_picked_twqflowbstd_none_po_kernel(
         nc.scalar.activation(quarter[:], sixteen[:], ACT.Abs_reciprocal_sqrt)
         ident = keep.tile([P, P], F32, name="ident")
         make_identity(nc, ident[:])
-        y_wide = [keep.tile([P, 2 * S], F32, name="y_wide%d" % t) for t in range(SLOTS)]
-        d_wide = [keep.tile([P, 2 * S], F32, name="d_wide%d" % t) for t in range(SLOTS)]
-        for t in range(SLOTS):
-            nc.vector.memset(y_wide[t][:, S:], 0.0)
-            nc.gpsimd.memset(d_wide[t][:, S:], 0.0)
         half_gs = keep.tile([P, SLOTS], F32, name="half_gs")
         nc.gpsimd.tensor_scalar(half_gs[:], gs_slots[:], 0.5, 0.0, ALU.mult, ALU.add)
 
@@ -145,6 +144,7 @@ def tile_picked_twqflowbstd_none_po_kernel(
 
         def project(token_words, token_scales, w_words, w_scales):
             banks = [slot_psum.tile([P, S], F32, name="slot_bank") for t in range(SLOTS)]
+            sorted_blocks = []
             for start in range(0, S, P):
                 tokens = slice(start, start + P)
                 by_token = work_psum.tile([P, H], F32, name="work_bank")
@@ -152,30 +152,33 @@ def tile_picked_twqflowbstd_none_po_kernel(
                     by_token[:], token_words[:, tokens].bitcast(FP8X4), token_scales[:, tokens],
                     w_words[:].bitcast(FP4X4), w_scales[:], start=True, stop=True,
                 )
-                sorted_by_slot = ring.tile([P, SLOTS, P], F32, name="sorted_by_slot")
+                sorted_by_slot = ring.tile([P, SLOTS, P], F32, name="sorted_by_slot", bufs=S // P)
                 nc.scalar.copy(sorted_by_slot[:], by_token[:].rearrange("c (m t) -> c t m", t=SLOTS))
-                for t in range(SLOTS):
+                sorted_blocks.append((tokens, sorted_by_slot))
+            for t in range(SLOTS):
+                for tokens, sorted_by_slot in sorted_blocks:
                     nc.tensor.transpose(banks[t][:, tokens], sorted_by_slot[:, t, :], ident[:])
             return banks
 
         y_banks = project(y_token_words, y_token_scales, w1_word_tile, w1_scale_tile)
-        y_narrow = [keep.tile([P, S], F32, name="y_narrow%d" % t) for t in range(SLOTS)]
+        y = [keep.tile([P, S], F32, name="y%d" % t) for t in range(SLOTS)]
+        y_again = [keep.tile([P, S], F32, name="y_again%d" % t) for t in range(SLOTS)]
         for t in range(SLOTS):
-            nc.scalar.copy(y_wide[t][:, :S], y_banks[t][:])
-            nc.scalar.copy(y_narrow[t][:], y_banks[t][:])
+            nc.scalar.copy(y[t][:], y_banks[t][:])
+            nc.scalar.copy(y_again[t][:], y_banks[t][:])
         d_banks = project(d_token_words, d_token_scales, w2_word_tile, w2_scale_tile)
+        half_gs_d = [keep.tile([P, S], F32, name="half_gs_d%d" % t) for t in range(SLOTS)]
         for t in range(SLOTS):
-            nc.scalar.activation(d_wide[t][:, :S], d_banks[t][:], ACT.Copy, scale=half_gs[:, t : t + 1])
-
-        diff2 = keep.tile([P, SLOTS, S], F32, name="diff2")
-        far = keep.tile([P, SLOTS, S], F32, name="far")
-        for t in range(SLOTS):
-            nc.vector.tensor_tensor(diff2[:, t, :], y_wide[t][:].indirect(n2_list[:]), y_narrow[t][:], ALU.subtract)
+            nc.scalar.activation(half_gs_d[t][:], d_banks[t][:], ACT.Copy, scale=half_gs[:, t : t + 1])
 
         z_codes = keep.tile([P, S], U32, name="z_codes", align_bytes=64)
         z_scales = keep.tile([P, S], U8, name="z_scales", align_bytes=64)
         h_banks = [slot_psum.tile([P, S], F32, name="slot_bank") for t in range(SLOTS)]
         h = [keep.tile([P, S], F32, name="h%d" % t) for t in range(SLOTS)]
+
+        h_centred = keep.tile([P, SLOTS, LAST_START], F32, name="h_centred")
+        h_to_spread = keep.tile([P, SLOTS, LAST_START], F32, name="h_to_spread")
+        h_spread = keep.tile([P, SLOTS, LAST_WIDTH], F32, name="h_spread")
 
         def make_h(start, n):
             cols = slice(start, start + n)
@@ -187,13 +190,16 @@ def tile_picked_twqflowbstd_none_po_kernel(
                 )
             for t in range(SLOTS):
                 nc.scalar.activation(h[t][:, cols], h_banks[t][:, cols], ACT.Copy, scale=H_SCALE)
+            if start < LAST_START:
+                for t in range(SLOTS):
+                    nc.scalar.activation(h_centred[:, t, cols], h_banks[t][:, cols], ACT.Copy, scale=H_IN_CENTRED * H_SCALE)
 
-        def add_and_round_turned(z_bf16, own, start, j):
+        def add_and_round_turned(z_bf16, own, far, j):
             block = slice(j * P, (j + 1) * P)
             pool, name = (first_psum, "first_bank") if j == 0 else (work_psum, "work_bank")
             z_turned = pool.tile([P, SLOTS, P], F32, name=name)
             for t in range(SLOTS):
-                add_transposed(z_turned[:, t, :], [far[:, t, start + j * P : start + (j + 1) * P], own[:, t, block]])
+                add_transposed(z_turned[:, t, :], [own[:, t, block], far[:, t, block]])
             pairs = ring.tile([P, 2, P, 2], BF16, name="pairs")
             nc.scalar.copy(pairs[:], z_turned[:].rearrange("c (u e) p -> c u p e", e=2))
             pair_words = pairs[:].rearrange("c u p e -> c (u p e)").bitcast(F32)
@@ -207,69 +213,90 @@ def tile_picked_twqflowbstd_none_po_kernel(
 
         for i, (start, n) in enumerate(PIECES):
             cols = slice(start, start + n)
-            last = i == len(PIECES) - 1
-            diff1 = keep.tile([P, SLOTS, n], F32, name="diff1", align_bytes=64)
-            own = keep.tile([P, SLOTS, n], F32, name="z_bf16_0" if last else "own%d" % i, align_bytes=64)
+            last = start == LAST_START
+            diff2 = keep.tile([P, SLOTS, n], F32, name="diff2", bufs=2)
+            if last:
+                diff1 = keep.tile([P, SLOTS, n], F32, name="z_bf16_0", align_bytes=64)
+            else:
+                diff1 = keep.tile([P, SLOTS, n], F32, name="diff1", bufs=2)
+            own = keep.tile([P, SLOTS, n], F32, name="own%d" % i)
             z_bf16 = keep.tile([P, n, SLOTS], BF16, name="z_bf16_%d" % i, align_bytes=64)
+            far = keep.tile([P, SLOTS, n], F32, name="z_bf16_1" if last else "far%d" % i, align_bytes=64)
+            for lst, diff in ((n2_list, diff2), (n1_list, diff1)):
+                for t in range(SLOTS):
+                    nc.vector.tensor_tensor(
+                        diff[:, t, :], y[t][:].indirect(entries(lst, start, n)), y_again[t][:, cols], ALU.subtract
+                    )
+            for t in range(SLOTS):
+                nc.vector.scalar_tensor_tensor(own[:, t, :], diff1[:, t, :], 2.0, half_gs_d[t][:, cols], ALU.mult, ALU.mult)
             for t in range(SLOTS):
                 nc.vector.tensor_tensor(
-                    diff1[:, t, :], y_narrow[t][:].indirect(entries(n1_list, start, n)), y_wide[t][:, cols], ALU.subtract
+                    far[:, t, :], half_gs_d[t][:].indirect(entries(n3_list, start, n)), diff2[:, t, :], ALU.mult
                 )
-            if i == 0:
-                for t in range(SLOTS):
-                    nc.vector.tensor_tensor(far[:, t, :], d_wide[t][:].indirect(n3_list[:]), diff2[:, t, :], ALU.mult)
-            for t in range(SLOTS):
-                nc.vector.scalar_tensor_tensor(own[:, t, :], diff1[:, t, :], 2.0, d_wide[t][:, cols], ALU.mult, ALU.mult)
             if last:
-                z_last = keep.tile([P, SLOTS, n], F32, name="z_last")
-                nc.vector.tensor_tensor(z_last[:], own[:], far[:, :, cols], ALU.add)
-                side_by_side(nc.vector.tensor_copy, z_bf16[:], z_last[:])
+                nc.vector.tensor_tensor(as_columns(z_bf16[:]), as_slots(own[:]), as_slots(far[:]), ALU.add)
             else:
                 for j in range(n // P):
-                    add_and_round_turned(z_bf16, own, start, j)
+                    add_and_round_turned(z_bf16, own, far, j)
             nc.vector.quantize_mx(z_codes[:, cols].bitcast(FP8X4), z_scales[:, cols], z_bf16[:].rearrange("p c t -> p (c t)"))
             if i > 0:
                 make_h(*PIECES[i - 1])
         make_h(*PIECES[-1])
-        h_part = keep.tile([P, SLOTS, S], F32, name="h_part")
         for t in range(SLOTS):
-            nc.scalar.activation(h_part[:, t, :], h_banks[t][:], ACT.Copy, scale=H_IN_SPREAD * H_SCALE)
+            nc.scalar.activation(
+                h_to_spread[:, t, :], h_banks[t][:, :LAST_START], ACT.Copy, scale=(H_IN_SPREAD - H_IN_CENTRED) * H_SCALE
+            )
+        for t in range(SLOTS):
+            nc.scalar.activation(h_spread[:, t, :], h_banks[t][:, LAST_START:], ACT.Copy, scale=H_IN_SPREAD * H_SCALE)
 
         out_slots = out_0.rearrange("(p t) c -> p t c", t=SLOTS)
         out_words = out_1[0].rearrange("p c r -> p (c r)").bitcast(I32)
         out_codes = keep.tile([P, S], I32, name="out_codes", align_bytes=64)
         out_scales = keep.tile([P, S], U8, name="out_scales", align_bytes=64)
         result = dict((start, keep.tile([P, SLOTS, n], F32, name="result%d" % start)) for start, n in PIECES)
-        for start, n, t0, count in STEPS:
+        for k, (start, n, t0, count) in enumerate(STEPS):
             cols = slice(start, start + n)
             slots = slice(t0, t0 + count)
-            blocks = [(a, j * P) for a in range(count) for j in range(n // P)]
-            pa = ring.tile([P, count, n], F32, name="pa", bufs=2)
-            gap = ring.tile([P, count, n], F32, name="gap")
-            both = ring.tile([P, count, n], F32, name="both")
-            centred = ring.tile([P, count, n], F32, name="centred")
-            for a in range(count):
-                nc.vector.tensor_copy(pa[:, a, :], h[t0 + a][:].indirect(entries(n4_list, start, n)))
-            for a in range(count):
-                nc.vector.tensor_tensor(both[:, a, :], h[t0 + a][:].indirect(entries(n5_list, start, n)), pa[:, a, :], ALU.add)
-            nc.vector.scalar_tensor_tensor(gap[:], pa[:], 2.0, both[:], ALU.mult, ALU.subtract)
-            nc.vector.scalar_tensor_tensor(centred[:], h_part[:, slots, cols], SPREAD_TO_CENTRED, both[:], ALU.mult, ALU.add)
+            by_n4, by_n5 = entries(n4_list, start, n), entries(n5_list, start, n)
+            if k == len(STEPS) - 1:
+                first = keep.tile([P, count, n], F32, name="centred1")
+            else:
+                first = ring.tile([P, count, n], F32, name="first", bufs=2)
+            second = keep.tile([P, count, n], F32, name="second%d" % k)
+            centred = keep.tile([P, count, n], F32, name="centred%d" % k)
+            if start < LAST_START:
+                for a in range(count):
+                    nc.vector.tensor_tensor(first[:, a, :], h[t0 + a][:].indirect(by_n4), h_centred[:, t0 + a, cols], ALU.add)
+                for a in range(count):
+                    nc.vector.tensor_tensor(second[:, a, :], h[t0 + a][:].indirect(by_n5), first[:, a, :], ALU.subtract)
+                nc.vector.scalar_tensor_tensor(centred[:], first[:], 2.0, second[:], ALU.mult, ALU.add)
+                terms = (
+                    (GAP_SCALE, (h_centred[:, slots, cols], second[:])),
+                    (SPREAD_SCALE, (h_to_spread[:, slots, cols], centred[:])),
+                )
+            else:
+                gap = keep.tile([P, count, n], F32, name="gap%d" % k)
+                for a in range(count):
+                    nc.vector.tensor_copy(first[:, a, :], h[t0 + a][:].indirect(by_n4))
+                for a in range(count):
+                    nc.vector.tensor_tensor(second[:, a, :], h[t0 + a][:].indirect(by_n5), first[:, a, :], ALU.add)
+                nc.vector.scalar_tensor_tensor(gap[:], first[:], 2.0, second[:], ALU.mult, ALU.subtract)
+                nc.vector.scalar_tensor_tensor(
+                    centred[:], h_spread[:, slots, :], H_IN_CENTRED / H_IN_SPREAD, second[:], ALU.mult, ALU.add
+                )
+                terms = ((SPREAD_SCALE, (h_spread[:, slots, :], second[:])), (GAP_SCALE, (gap[:],)))
 
+            blocks = [(a, slice(c, c + P)) for a in range(count) for c in range(0, n, P)]
             squares = ring.tile([P, 2, count, n], F32, name="squares")
             inverse_root = ring.tile([P, count, n], F32, name="inverse_root")
-            spread_turned = slot_psum.tile([P, count, n], F32, name="slot_bank")
-            for a, c in blocks:
-                add_transposed(
-                    spread_turned[:, a, c : c + P], [h_part[:, t0 + a, start + c : start + c + P], both[:, a, c : c + P]]
-                )
-            nc.scalar.activation(squares[:, 1], spread_turned[:], ACT.Square, scale=SPREAD_SCALE)
-            gap_turned = slot_psum.tile([P, count, n], F32, name="slot_bank")
-            for a, c in blocks:
-                add_transposed(gap_turned[:, a, c : c + P], [gap[:, a, c : c + P]])
-            nc.scalar.activation(squares[:, 0], gap_turned[:], ACT.Square, scale=GAP_SCALE)
+            for e, (scale, parts) in enumerate(terms):
+                term_turned = slot_psum.tile([P, count, n], F32, name="slot_bank")
+                for a, block in blocks:
+                    add_transposed(term_turned[:, a, block], [part[:, a, block] for part in parts])
+                nc.scalar.activation(squares[:, e], term_turned[:], ACT.Square, scale=scale)
             total = work_psum.tile([P, count, n], F32, name="work_bank")
-            for a, c in blocks:
-                add_transposed(total[:, a, c : c + P], [squares[:, 1, a, c : c + P], squares[:, 0, a, c : c + P]])
+            for a, block in blocks:
+                add_transposed(total[:, a, block], [squares[:, 0, a, block], squares[:, 1, a, block]])
             nc.scalar.activation(inverse_root[:], total[:], ACT.Abs_reciprocal_sqrt, bias=quarter[:])
             nc.vector.scalar_tensor_tensor(
                 result[start][:, slots, :], centred[:], -MU_SCALE, inverse_root[:], ALU.mult, ALU.mult
@@ -278,13 +305,14 @@ def tile_picked_twqflowbstd_none_po_kernel(
             if t0 + count == SLOTS:
                 nc.sync.dma_start(out_slots[:, :, cols], result[start][:])
                 out_bf16 = keep.tile([P, n, SLOTS], BF16, name="out_bf16_%d" % start, align_bytes=64)
-                side_by_side(nc.scalar.copy if start == 0 else nc.vector.tensor_copy, out_bf16[:], result[start][:])
+                round_copy = nc.scalar.copy if start == 0 else nc.vector.tensor_copy
+                round_copy(as_columns(out_bf16[:]), as_slots(result[start][:]))
                 nc.vector.quantize_mx(
                     out_codes[:, cols].bitcast(FP8X4), out_scales[:, cols], out_bf16[:].rearrange("p c t -> p (c t)")
                 )
                 nc.sync.dma_start(out_words[:, cols], out_codes[:, cols])
         for quad in range(P // QUADRANT):
-            nc.sync.dma_start(
+            (nc.scalar if quad % 2 == 0 else nc.sync).dma_start(
                 out_2[0].bitcast(I32)[4 * quad : 4 * quad + 4, :],
                 out_scales[QUADRANT * quad : QUADRANT * quad + 4, :].bitcast(I32),
             )

from contextlib import ExitStack

import concourse.mybir as mybir
from concourse.masks import make_identity

K, T, S, H, G = 512, 1024, 512, 512, 2048
FLOPS = 3 * 2 * K * H * S

F32 = mybir.dt.float32
BF16 = mybir.dt.bfloat16
I32 = mybir.dt.int32
U32 = mybir.dt.uint32
U16 = mybir.dt.uint16
U8 = mybir.dt.uint8
FP8X4 = mybir.dt.float8_e4m3fn_x4
FP4X4 = mybir.dt.float4_e2m1fn_x4
ALU = mybir.AluOpType
ACT = mybir.ActivationFunctionType

P = 128
SLOTS = 4
PER_COLUMN = 16
QUADRANT = 32
PIECES = ((0, 256), (256, 128), (384, 128))
STEPS = ((0, 256, 0, 2), (0, 256, 2, 2), (256, 128, 0, 4), (384, 128, 0, 2), (384, 128, 2, 2))
LAST_START, LAST_WIDTH = PIECES[-1]

H_SCALE = 0.0625
MU_SCALE = 0.3125
H_IN_CENTRED = -11.0 / 5.0
H_IN_SPREAD = -5.0 / 3.0
GAP_SCALE = 0.5**0.5
SPREAD_SCALE = 0.375 * 0.5**0.5


def tile_picked_twqflowbstd_none_po_kernel(
    tc, x_words, x_scales, w1_words, w1_scales, w2_words, w2_scales, gs, d_words, d_scales,
    offs, two, n1, n2, n3, k1, n4, n5, out_0, out_1, out_2,
):
    nc = tc.nc
    with ExitStack() as ctx:
        keep = ctx.enter_context(tc.tile_pool(name="keep", bufs=1))
        ring = ctx.enter_context(tc.tile_pool(name="ring", bufs=3))
        slot_psum = ctx.enter_context(tc.psum_pool(name="slot_psum", bufs=SLOTS))
        first_psum = ctx.enter_context(tc.psum_pool(name="first_psum", bufs=1))
        work_psum = ctx.enter_context(tc.psum_pool(name="work_psum", bufs=3))

        def load_list(name, src):
            tile = keep.tile([P, S // PER_COLUMN], U16, name=name)
            nc.sync.dma_start(tile[:], src)
            return tile

        def entries(lst, start, n):
            return lst[:, start // PER_COLUMN : (start + n) // PER_COLUMN]

        def zeroed_scales(name, width, engine):
            tile = keep.tile([P, width], U8, name=name, align_bytes=64)
            engine.memset(tile[:].bitcast(I32), 0)
            return tile

        def load_scales(tile, scales, places):
            rows = scales[0].bitcast(I32).rearrange("(q r) c -> r q c", r=4)
            for r, place in enumerate(places):
                nc.sync.dma_start(tile[place:P:QUADRANT, :].bitcast(I32), rows[r])

        def load_words(name, words, width):
            tile = keep.tile([P, width], I32, name=name)
            nc.sync.dma_start(tile[:], words[0].rearrange("p c r -> p (c r)").bitcast(I32))
            return tile

        def load_fp4(name, words):
            tile = keep.tile([P, 2 * H], U8, name=name, align_bytes=64)
            nc.sync.dma_start(tile[:].bitcast(I32), words[0].bitcast(I32))
            return tile

        def add_transposed(out, parts):
            for i, part in enumerate(parts):
                nc.tensor.matmul(out, part, ident[:], is_transpose=True, start=(i == 0), stop=(i == len(parts) - 1))

        def as_columns(tile):
            return tile.rearrange("p (c i) t -> p c t i", i=4)

        def as_slots(tile):
            return tile.rearrange("p t (c i) -> p c t i", i=4)

        x_scale_table = zeroed_scales("x_scale_table", T, nc.gpsimd)
        w1_scale_tile = zeroed_scales("w1_scale_tile", H, nc.vector)
        d_scale_table = zeroed_scales("d_scale_table", G, nc.vector)
        w2_scale_tile = zeroed_scales("w2_scale_tile", H, nc.vector)
        code_scales = zeroed_scales("code_scales", H, nc.vector)
        in_place = (0, 1, 2, 3)
        by_run = (0, 1, 16, 17)

        offs_list = load_list("offs_list", offs)
        x_word_table = load_words("x_word_table", x_words, T)
        load_scales(x_scale_table, x_scales, in_place)
        w1_word_tile = load_fp4("w1_word_tile", w1_words)
        two_list = load_list("two_list", two)
        load_scales(w1_scale_tile, w1_scales, in_place)
        k1_list = load_list("k1_list", k1)
        d_word_table = load_words("d_word_table", d_words, G)
        load_scales(d_scale_table, d_scales, by_run)
        w2_word_tile = load_fp4("w2_word_tile", w2_words)
        load_scales(w2_scale_tile, w2_scales, in_place)
        n2_list = load_list("n2_list", n2)
        n1_list = load_list("n1_list", n1)
        gs_slots = keep.tile([P, SLOTS], F32, name="gs_slots")
        nc.sync.dma_start(gs_slots[:], gs.rearrange("(p t) o -> p (t o)", t=SLOTS))
        n3_list = load_list("n3_list", n3)
        n4_list = load_list("n4_list", n4)
        n5_list = load_list("n5_list", n5)

        sixteen = keep.tile([P, 1], F32, name="sixteen")
        nc.gpsimd.memset(sixteen[:], 16.0)
        quarter = keep.tile([P, 1], F32, name="quarter")
        nc.scalar.activation(quarter[:], sixteen[:], ACT.Abs_reciprocal_sqrt)
        ident = keep.tile([P, P], F32, name="ident")
        make_identity(nc, ident[:])
        half_gs = keep.tile([P, SLOTS], F32, name="half_gs")
        nc.gpsimd.tensor_scalar(half_gs[:], gs_slots[:], 0.5, 0.0, ALU.mult, ALU.add)

        def pick(name, word_table, scale_table, lst, n):
            words = keep.tile([P, S], I32, name=name + "_words", align_bytes=64)
            scales = keep.tile([P, S], U8, name=name + "_scales", align_bytes=64)
            for start in range(0, S, n):
                part = entries(lst, start, n)
                nc.vector.tensor_copy(words[:, start : start + n].bitcast(U32), word_table[:].bitcast(U32).indirect(part))
                nc.vector.tensor_copy(scales[:, start : start + n], scale_table[:].indirect(part))
            return words, scales

        y_token_words, y_token_scales = pick("y_token", x_word_table, x_scale_table, offs_list, S // 2)
        d_token_words, d_token_scales = pick("d_token", x_word_table, x_scale_table, two_list, S)
        picked_words, picked_scales = pick("picked", d_word_table, d_scale_table, k1_list, S)
        code_words = keep.tile([P, H], I32, name="code_words", align_bytes=64)
        nc.vector.tensor_copy(
            code_words[:].rearrange("p (t m) -> p t m", t=SLOTS), picked_words[:].rearrange("p (m t) -> p t m", t=SLOTS)
        )
        dealt_scales = keep.tile([P, H], U8, name="dealt_scales")
        nc.vector.tensor_copy(
            dealt_scales[:].rearrange("p (t m) -> p t m", t=SLOTS), picked_scales[:].rearrange("p (m t) -> p t m", t=SLOTS)
        )
        for r, place in enumerate(by_run):
            nc.sync.dma_start(code_scales[r:P:QUADRANT, :].bitcast(I32), dealt_scales[place:P:QUADRANT, :].bitcast(I32))

        def project(token_words, token_scales, w_words, w_scales):
            banks = [slot_psum.tile([P, S], F32, name="slot_bank") for t in range(SLOTS)]
            sorted_blocks = []
            for start in range(0, S, P):
                tokens = slice(start, start + P)
                by_token = work_psum.tile([P, H], F32, name="work_bank")
                nc.tensor.matmul_mx(
                    by_token[:], token_words[:, tokens].bitcast(FP8X4), token_scales[:, tokens],
                    w_words[:].bitcast(FP4X4), w_scales[:], start=True, stop=True,
                )
                sorted_by_slot = ring.tile([P, SLOTS, P], F32, name="sorted_by_slot", bufs=S // P)
                nc.scalar.copy(sorted_by_slot[:], by_token[:].rearrange("c (m t) -> c t m", t=SLOTS))
                sorted_blocks.append((tokens, sorted_by_slot))
            for t in range(SLOTS):
                for tokens, sorted_by_slot in sorted_blocks:
                    nc.tensor.transpose(banks[t][:, tokens], sorted_by_slot[:, t, :], ident[:])
            return banks

        y_banks = project(y_token_words, y_token_scales, w1_word_tile, w1_scale_tile)
        y = [keep.tile([P, S], F32, name="y%d" % t) for t in range(SLOTS)]
        y_again = [keep.tile([P, S], F32, name="y_again%d" % t) for t in range(SLOTS)]
        for t in range(SLOTS):
            nc.scalar.copy(y[t][:], y_banks[t][:])
            nc.scalar.copy(y_again[t][:], y_banks[t][:])
        d_banks = project(d_token_words, d_token_scales, w2_word_tile, w2_scale_tile)
        half_gs_d = [keep.tile([P, S], F32, name="half_gs_d%d" % t) for t in range(SLOTS)]
        for t in range(SLOTS):
            nc.scalar.activation(half_gs_d[t][:], d_banks[t][:], ACT.Copy, scale=half_gs[:, t : t + 1])

        z_codes = keep.tile([P, S], U32, name="z_codes", align_bytes=64)
        z_scales = keep.tile([P, S], U8, name="z_scales", align_bytes=64)
        h_banks = [slot_psum.tile([P, S], F32, name="slot_bank") for t in range(SLOTS)]
        h = [keep.tile([P, S], F32, name="h%d" % t) for t in range(SLOTS)]

        h_centred = keep.tile([P, SLOTS, LAST_START], F32, name="h_centred")
        h_to_spread = keep.tile([P, SLOTS, LAST_START], F32, name="h_to_spread")
        h_spread = keep.tile([P, SLOTS, LAST_WIDTH], F32, name="h_spread")

        def make_h(start, n):
            cols = slice(start, start + n)
            for t in range(SLOTS):
                features = slice(t * P, (t + 1) * P)
                nc.tensor.matmul_mx(
                    h_banks[t][:, cols], code_words[:, features].bitcast(FP8X4), code_scales[:, features],
                    z_codes[:, cols].bitcast(FP8X4), z_scales[:, cols], start=True, stop=True,
                )
            for t in range(SLOTS):
                nc.scalar.activation(h[t][:, cols], h_banks[t][:, cols], ACT.Copy, scale=H_SCALE)
            if start < LAST_START:
                for t in range(SLOTS):
                    nc.scalar.activation(h_centred[:, t, cols], h_banks[t][:, cols], ACT.Copy, scale=H_IN_CENTRED * H_SCALE)

        def add_and_round_turned(z_bf16, own, far, j):
            block = slice(j * P, (j + 1) * P)
            pool, name = (first_psum, "first_bank") if j == 0 else (work_psum, "work_bank")
            z_turned = pool.tile([P, SLOTS, P], F32, name=name)
            for t in range(SLOTS):
                add_transposed(z_turned[:, t, :], [own[:, t, block], far[:, t, block]])
            pairs = ring.tile([P, 2, P, 2], BF16, name="pairs")
            nc.scalar.copy(pairs[:], z_turned[:].rearrange("c (u e) p -> c u p e", e=2))
            pair_words = pairs[:].rearrange("c u p e -> c (u p e)").bitcast(F32)
            pairs_back = work_psum.tile([P, 2, P], F32, name="work_bank")
            for u in range(2):
                nc.tensor.transpose(pairs_back[:, u, :], pair_words[:, u * P : (u + 1) * P], ident[:])
            nc.scalar.copy(
                z_bf16[:, block, :].rearrange("p c t -> p (c t)").bitcast(F32).rearrange("p (c u) -> p c u", u=2),
                pairs_back[:].rearrange("p u c -> p c u"),
            )

        for i, (start, n) in enumerate(PIECES):
            cols = slice(start, start + n)
            last = start == LAST_START
            diff2 = keep.tile([P, SLOTS, n], F32, name="diff2", bufs=2)
            if last:
                diff1 = keep.tile([P, SLOTS, n], F32, name="z_bf16_0", align_bytes=64)
            else:
                diff1 = keep.tile([P, SLOTS, n], F32, name="diff1", bufs=2)
            own = keep.tile([P, SLOTS, n], F32, name="own%d" % i)
            z_bf16 = keep.tile([P, n, SLOTS], BF16, name="z_bf16_%d" % i, align_bytes=64)
            far = keep.tile([P, SLOTS, n], F32, name="z_bf16_1" if last else "far%d" % i, align_bytes=64)
            for lst, diff in ((n2_list, diff2), (n1_list, diff1)):
                for t in range(SLOTS):
                    nc.vector.tensor_tensor(
                        diff[:, t, :], y[t][:].indirect(entries(lst, start, n)), y_again[t][:, cols], ALU.subtract
                    )
            for t in range(SLOTS):
                nc.vector.scalar_tensor_tensor(own[:, t, :], diff1[:, t, :], 2.0, half_gs_d[t][:, cols], ALU.mult, ALU.mult)
            for t in range(SLOTS):
                nc.vector.tensor_tensor(
                    far[:, t, :], half_gs_d[t][:].indirect(entries(n3_list, start, n)), diff2[:, t, :], ALU.mult
                )
            if last:
                nc.vector.tensor_tensor(as_columns(z_bf16[:]), as_slots(own[:]), as_slots(far[:]), ALU.add)
            else:
                for j in range(n // P):
                    add_and_round_turned(z_bf16, own, far, j)
            nc.vector.quantize_mx(z_codes[:, cols].bitcast(FP8X4), z_scales[:, cols], z_bf16[:].rearrange("p c t -> p (c t)"))
            if i > 0:
                make_h(*PIECES[i - 1])
        make_h(*PIECES[-1])
        for t in range(SLOTS):
            nc.scalar.activation(
                h_to_spread[:, t, :], h_banks[t][:, :LAST_START], ACT.Copy, scale=(H_IN_SPREAD - H_IN_CENTRED) * H_SCALE
            )
        for t in range(SLOTS):
            nc.scalar.activation(h_spread[:, t, :], h_banks[t][:, LAST_START:], ACT.Copy, scale=H_IN_SPREAD * H_SCALE)

        out_slots = out_0.rearrange("(p t) c -> p t c", t=SLOTS)
        out_words = out_1[0].rearrange("p c r -> p (c r)").bitcast(I32)
        out_codes = keep.tile([P, S], I32, name="out_codes", align_bytes=64)
        out_scales = keep.tile([P, S], U8, name="out_scales", align_bytes=64)
        result = dict((start, keep.tile([P, SLOTS, n], F32, name="result%d" % start)) for start, n in PIECES)
        for k, (start, n, t0, count) in enumerate(STEPS):
            cols = slice(start, start + n)
            slots = slice(t0, t0 + count)
            by_n4, by_n5 = entries(n4_list, start, n), entries(n5_list, start, n)
            if k == len(STEPS) - 1:
                first = keep.tile([P, count, n], F32, name="centred1")
            else:
                first = ring.tile([P, count, n], F32, name="first", bufs=2)
            second = keep.tile([P, count, n], F32, name="second%d" % k)
            centred = keep.tile([P, count, n], F32, name="centred%d" % k)
            if start < LAST_START:
                for a in range(count):
                    nc.vector.tensor_tensor(first[:, a, :], h[t0 + a][:].indirect(by_n4), h_centred[:, t0 + a, cols], ALU.add)
                for a in range(count):
                    nc.vector.tensor_tensor(second[:, a, :], h[t0 + a][:].indirect(by_n5), first[:, a, :], ALU.subtract)
                nc.vector.scalar_tensor_tensor(centred[:], first[:], 2.0, second[:], ALU.mult, ALU.add)
                terms = (
                    (GAP_SCALE, (h_centred[:, slots, cols], second[:])),
                    (SPREAD_SCALE, (h_to_spread[:, slots, cols], centred[:])),
                )
            else:
                gap = keep.tile([P, count, n], F32, name="gap%d" % k)
                for a in range(count):
                    nc.vector.tensor_copy(first[:, a, :], h[t0 + a][:].indirect(by_n4))
                for a in range(count):
                    nc.vector.tensor_tensor(second[:, a, :], h[t0 + a][:].indirect(by_n5), first[:, a, :], ALU.add)
                nc.vector.scalar_tensor_tensor(gap[:], first[:], 2.0, second[:], ALU.mult, ALU.subtract)
                nc.vector.scalar_tensor_tensor(
                    centred[:], h_spread[:, slots, :], H_IN_CENTRED / H_IN_SPREAD, second[:], ALU.mult, ALU.add
                )
                terms = ((SPREAD_SCALE, (h_spread[:, slots, :], second[:])), (GAP_SCALE, (gap[:],)))

            blocks = [(a, slice(c, c + P)) for a in range(count) for c in range(0, n, P)]
            squares = ring.tile([P, 2, count, n], F32, name="squares")
            inverse_root = ring.tile([P, count, n], F32, name="inverse_root")
            for e, (scale, parts) in enumerate(terms):
                term_turned = slot_psum.tile([P, count, n], F32, name="slot_bank")
                for a, block in blocks:
                    add_transposed(term_turned[:, a, block], [part[:, a, block] for part in parts])
                nc.scalar.activation(squares[:, e], term_turned[:], ACT.Square, scale=scale)
            total = work_psum.tile([P, count, n], F32, name="work_bank")
            for a, block in blocks:
                add_transposed(total[:, a, block], [squares[:, 0, a, block], squares[:, 1, a, block]])
            nc.scalar.activation(inverse_root[:], total[:], ACT.Abs_reciprocal_sqrt, bias=quarter[:])
            nc.vector.scalar_tensor_tensor(
                result[start][:, slots, :], centred[:], -MU_SCALE, inverse_root[:], ALU.mult, ALU.mult
            )

            if t0 + count == SLOTS:
                nc.sync.dma_start(out_slots[:, :, cols], result[start][:])
                out_bf16 = keep.tile([P, n, SLOTS], BF16, name="out_bf16_%d" % start, align_bytes=64)
                round_copy = nc.scalar.copy if start == 0 else nc.vector.tensor_copy
                round_copy(as_columns(out_bf16[:]), as_slots(result[start][:]))
                nc.vector.quantize_mx(
                    out_codes[:, cols].bitcast(FP8X4), out_scales[:, cols], out_bf16[:].rearrange("p c t -> p (c t)")
                )
                nc.sync.dma_start(out_words[:, cols], out_codes[:, cols])
        for quad in range(P // QUADRANT):
            (nc.scalar if quad % 2 == 0 else nc.sync).dma_start(
                out_2[0].bitcast(I32)[4 * quad : 4 * quad + 4, :],
                out_scales[QUADRANT * quad : QUADRANT * quad + 4, :].bitcast(I32),
            )
